import numpy as np
import ml_dtypes


def mxq(x, axis, fmt="e4m3"):
    dtype, down = {"e4m3": (ml_dtypes.float8_e4m3fn, 7), "e5m2": (ml_dtypes.float8_e5m2, 14)}[fmt]
    v = np.moveaxis(np.asarray(x, np.float32).astype(ml_dtypes.bfloat16).astype(np.float64), axis, -1)
    blocks = v.reshape(v.shape[:-1] + (-1, 32))
    amax = np.abs(blocks).max(-1, keepdims=True)
    byte = np.maximum(np.where(amax > 0, np.frexp(amax)[1] - 1 + 127, 0) - down, 1)
    scale = np.exp2(byte - 127.0)
    codes = (blocks / scale).astype(np.float32).astype(dtype).astype(np.float64)
    return np.moveaxis((codes * scale).reshape(v.shape), -1, axis)


WIDE = False


def mx_kscale(k):
    if not WIDE:
        return np.ones(k)
    levels = np.array([10, -10, 5, -5, 0])
    if k % 512:
        return np.exp2(np.random.permutation(np.resize(levels, k // 32))).repeat(32)
    a = np.empty((k // 512, 16))
    for p in range(k // 512):
        a[p, :8] = np.random.permutation(np.resize(levels, 8))
        for g in range(8):
            far = levels[np.abs(levels - a[p, g]) >= 10]
            a[p, g + 8] = far[np.random.randint(len(far))]
    return np.exp2(a.ravel()).repeat(32)


BF16 = ml_dtypes.bfloat16


def bf(x):
    return np.asarray(x, np.float32).astype(BF16)


def f64(x):
    return np.asarray(x).astype(np.float64)


T, DI, DO, R = 2048, 1024, 1024, 256


def draw0():
    s, t = mx_kscale(T), mx_kscale(DO)
    return {"x": bf((0.3 + np.random.standard_normal((T, DI))) * s[:, None]),
            "g": bf(np.random.standard_normal((T, DO)) / np.sqrt(T) / s[:, None]),
            "v": bf((0.5 + np.random.standard_normal((DI, DO))) / np.sqrt(DI)),
            "m": bf((1.0 + 0.1 * np.random.standard_normal(DO)) * t),
            "b": bf(np.random.standard_normal((R, DO)) / np.sqrt(DO) / t[None, :])}


def unit_columns(v):
    n = np.sqrt(np.sum(v * v, axis=0))
    u = v / n[None, :]
    return n, u


def core(x, g, v, m, b):
    n, u = unit_columns(f64(v))
    gw = mxq(f64(x), 0, "e4m3").T @ mxq(f64(g), 0, "e4m3")
    c = np.sum(u * gw, axis=0)
    dv = (f64(m) / n)[None, :] * (gw - u * c[None, :])
    return mxq(dv, 1, "e4m3") @ mxq(f64(b), 1, "e4m3").T


def e4m3fn_bytes(y):
    return np.clip(np.asarray(y, np.float64), -448.0, 448.0).astype(np.float32).astype(ml_dtypes.float8_e4m3fn).view(np.uint8)


def e4m3fn_values(b):
    return np.asarray(b, np.uint8).view(ml_dtypes.float8_e4m3fn).astype(np.float64)


def setup_inputs():
    d = draw0()
    x0 = np.asarray(d['x']).astype(np.float64)
    s = (np.max(np.abs(x0), axis=(1,), keepdims=True) / 448.0).astype(np.float32)
    out = {}
    for k, v in d.items():
        if k == 'x':
            out['x_bytes'] = e4m3fn_bytes(x0 / s.astype(np.float64))
            out['x_scale'] = s
        else:
            out[k] = v
    return out


def reference(x_bytes, x_scale, g, v, m, b):
    return core(e4m3fn_values(x_bytes) * x_scale.astype(np.float64), g, v, m, b)

@@ -1,0 +1,331 @@
+from contextlib import ExitStack
+
+import concourse.mybir as mybir
+from concourse.masks import make_identity
+
+T, DI, DO, R = 2048, 1024, 1024, 256
+FLOPS = 2 * T * DI * DO + 2 * DI * DO * R
+
+F32 = mybir.dt.float32
+BF16 = mybir.dt.bfloat16
+U32 = mybir.dt.uint32
+U8 = mybir.dt.uint8
+FP8 = mybir.dt.float8_e4m3fn
+FP8X4 = mybir.dt.float8_e4m3fn_x4
+ACT = mybir.ActivationFunctionType
+ALU = mybir.AluOpType
+
+P = 128
+PACK = 4
+KP = P * PACK
+NQ = T // KP
+NH = DO // KP
+HALF = 512
+NJ = NH * PACK
+CH = 256
+
+
+def tile_doradirectiongradienttoloradown_kernel(tc, x_bytes, x_scale, g, v, m, b, out):
+    nc = tc.nc
+    with ExitStack() as ctx:
+        keep = ctx.enter_context(tc.tile_pool(name="keep", bufs=1))
+        work = ctx.enter_context(tc.tile_pool(name="work", bufs=1))
+        psum = ctx.enter_context(tc.psum_pool(name="psum", bufs=1))
+        ctx.enter_context(tc.manual_schedule())
+
+        def kept(name, shape, dtype):
+            return keep.tile(shape, dtype, name=name, align_bytes=64)
+
+        def bank(k, name, shape, dtype):
+            return psum.tile(shape, dtype, name=name, tag="bank%d" % k)
+
+        xs = kept("xs", [P, NQ, PACK], F32)
+        m_sb = kept("m_sb", [P, NH, PACK], BF16)
+        xb0 = [kept("xbytes0_%d" % a, [P, PACK, HALF], U8) for a in range(2)]
+        xb = {q: kept("xbytes%d" % q, [P, PACK, DI], U8) for q in range(1, NQ)}
+        g_raw = {(h, q): kept("graw%d_%d" % (h, q), [P, PACK, KP], BF16) for h in range(NH) for q in range(NQ)}
+        v_sb = [kept("v%d" % h, [P, DI // P, KP], BF16) for h in range(NH)]
+        b_sb = kept("b_sb", [P, R // P, DO], BF16)
+        x_codes = [kept("xc%d" % q, [P, DI], U32) for q in range(NQ)]
+        x_scales = [kept("xsc%d" % q, [P, DI], U8) for q in range(NQ)]
+        g_codes = {k: kept("gc%d_%d" % k, [P, KP], U32) for k in g_raw}
+        g_scales = {k: kept("gsc%d_%d" % k, [P, KP], U8) for k in g_raw}
+        dv_codes = [kept("dc%d" % h, [P, DI], U32) for h in range(NH)]
+        dv_scales = [kept("dsc%d" % h, [P, DI], U8) for h in range(NH)]
+        b_codes = kept("bc", [P, NH * R], U32)
+        b_scales = kept("bsc", [P, NH * R], U8)
+        dv = {(h, a): kept("dv%d_%d" % (h, a), [P, PACK, HALF], BF16) for h in range(NH) for a in range(2)}
+        ident_bf = kept("ident_bf", [P, P], BF16)
+        ident_f = kept("ident_f", [P, P], F32)
+        one = kept("one", [P, 1], F32)
+        warm = kept("warm", [P, 1], F32)
+        n2 = [kept("n2_%d" % h, [P, PACK], F32) for h in range(NH)]
+        rn2 = [kept("rn2_%d" % h, [P, PACK], F32) for h in range(NH)]
+        rn = [kept("rn_%d" % h, [P, PACK], F32) for h in range(NH)]
+        nalpha = [kept("na_%d" % h, [P, PACK], F32) for h in range(NH)]
+        gam = kept("gam", [P, NJ], F32)
+
+        def load_x(q):
+            nc.sync.dma_start(out=xb[q][:], in_=x_bytes[q * KP:(q + 1) * KP, :].rearrange("(p j) w -> p j w", j=PACK))
+
+        def load_x0(a):
+            nc.sync.dma_start(out=xb0[a][:], in_=x_bytes[0:KP, a * HALF:(a + 1) * HALF].rearrange("(p j) w -> p j w", j=PACK))
+
+        def load_g(h, q):
+            nc.sync.dma_start(out=g_raw[h, q][:],
+                              in_=g[q * KP:(q + 1) * KP, h * KP:(h + 1) * KP].rearrange("(p j) w -> p j w", j=PACK))
+
+        def load_v(h):
+            nc.sync.dma_start(out=v_sb[h][:], in_=v[:, h * KP:(h + 1) * KP].rearrange("(a p) o -> p a o", p=P))
+
+        nc.sync.dma_start(out=xs[:], in_=x_scale.rearrange("(q p j) o -> p q (j o)", p=P, j=PACK))
+        load_x0(0)
+        load_g(0, 0)
+        load_x0(1)
+        load_x(1)
+        load_g(0, 1)
+        load_v(0)
+        load_x(2)
+        load_g(0, 2)
+        load_v(1)
+        load_g(1, 0)
+        load_x(3)
+        load_g(0, 3)
+        nc.sync.dma_start(out=m_sb[:], in_=m.rearrange("(h p t) -> p h t", p=P, t=PACK))
+        load_g(1, 1)
+        load_g(1, 2)
+        load_g(1, 3)
+        nc.sync.dma_start(out=b_sb[:], in_=b.rearrange("(c p) o -> p c o", p=P))
+
+        nc.gpsimd.memset(one[:], 1.0)
+        nc.scalar.activation(out=warm[:], in_=one[:], func=ACT.Sqrt)
+        make_identity(nc, ident_bf[:])
+        make_identity(nc, ident_f[:])
+
+        def copy(eng, out_ap, in_ap):
+            if eng == "V":
+                nc.vector.tensor_copy(out=out_ap, in_=in_ap)
+            else:
+                nc.scalar.copy(out=out_ap, in_=in_ap)
+
+        def quantize(codes, scales, src):
+            nc.vector.quantize_mx(out=codes.bitcast(FP8X4), scales=scales, in_=src)
+
+        def widen(q, a):
+            xw = work.tile([P, PACK, HALF], BF16, name="xw", bufs=4, align_bytes=64)
+            for j in range(PACK):
+                src = xb0[a][:, j, :] if q == 0 else xb[q][:, j, a * HALF:(a + 1) * HALF]
+                nc.scalar.activation(out=xw[:, j, :], in_=src.bitcast(FP8), func=ACT.Copy, scale=xs[:, q, j:j + 1])
+            return xw
+
+        def interleave(eng, planes, width, name, bufs):
+            il = work.tile([P, width * PACK], BF16, name=name, bufs=bufs, align_bytes=64)
+            copy(eng, il[:].rearrange("p (c i t) -> p c t i", i=4, t=PACK),
+                 planes.rearrange("p t (c i) -> p c t i", i=4))
+            return il
+
+        def interleave_g(eng, h, q, name, bufs):
+            il = work.tile([P, KP * PACK], BF16, name=name, bufs=bufs, align_bytes=64)
+            copy(eng, il[:].rearrange("p (t c e j) -> p c j e t", t=PACK, e=2, j=PACK),
+                 g_raw[h, q][:].rearrange("p j (c e t) -> p c j e t", e=2, t=PACK))
+            return il
+
+        def quantize_g(h, q, il):
+            quantize(g_codes[h, q][:], g_scales[h, q][:], il[:])
+
+        def quantize_x(q, a, il):
+            cols = slice(a * HALF, (a + 1) * HALF)
+            quantize(x_codes[q][:, cols], x_scales[q][:, cols], il[:])
+
+        acc = {}
+
+        def product(j, a, passes):
+            h, t = divmod(j, PACK)
+            if (j, a) not in acc:
+                acc[j, a] = bank(2 * (j % 2) + a, "acc", [P, HALF], F32)
+            oc = slice(t * P, (t + 1) * P)
+            ic = slice(a * HALF, (a + 1) * HALF)
+            for q in passes:
+                nc.tensor.matmul_mx(out=acc[j, a][:], lhsT=g_codes[h, q][:, oc].bitcast(FP8X4), lhsT_scale=g_scales[h, q][:, oc],
+                                    rhs=x_codes[q][:, ic].bitcast(FP8X4), rhs_scale=x_scales[q][:, ic],
+                                    start=(q == 0), stop=(q == NQ - 1))
+
+        def product_tile(j):
+            product(j, 0, range(NQ))
+            product(j, 1, range(NQ))
+
+        gram = {}
+
+        def gram_products(h):
+            gram[h] = bank(4 + h, "gram", [P, PACK, P], F32)
+            for t in range(PACK):
+                for c in range(DI // P):
+                    cols = v_sb[h][:, c, t:KP:PACK]
+                    nc.tensor.matmul(out=gram[h][:, t, :], lhsT=cols, rhs=cols, start=(c == 0), stop=(c == DI // P - 1))
+
+        def norms(h):
+            for t in range(PACK):
+                junk = work.tile([P, DI], F32, name="junk", bufs=2, align_bytes=64)
+                nc.vector.scalar_tensor_tensor(out=junk[:, 0:P], in0=gram[h][:, t, :], scalar=1.0, in1=ident_f[:],
+                                               op0=ALU.mult, op1=ALU.mult, accum_out=n2[h][:, t:t + 1])
+
+        def recip(h):
+            nc.vector.reciprocal(out=rn2[h][:], in_=n2[h][:])
+
+        def root(h):
+            nc.scalar.activation(out=rn[h][:], in_=rn2[h][:], func=ACT.Sqrt)
+
+        def alpha(h):
+            nc.vector.scalar_tensor_tensor(out=nalpha[h][:], in0=rn[h][:], scalar=-1.0, in1=m_sb[:, h, :],
+                                           op0=ALU.mult, op1=ALU.mult)
+
+        vt = {}
+
+        def turn_v(j):
+            h, t = divmod(j, PACK)
+            vt[j] = bank(4 + (j + 2) % 4, "vt", [P, DI], BF16)
+            for c in range(DI // P):
+                nc.tensor.transpose(vt[j][:, c * P:(c + 1) * P], v_sb[h][:, c, t:KP:PACK], ident_bf[:])
+
+        gs = {}
+
+        def scale_out(j):
+            h, t = divmod(j, PACK)
+            gs[j] = work.tile([P, DI], F32, name="gs", bufs=4, align_bytes=64)
+            for a in range(2):
+                nc.scalar.activation(out=gs[j][:, a * HALF:(a + 1) * HALF], in_=acc[j, a][:], func=ACT.Copy,
+                                     scale=nalpha[h][:, t:t + 1])
+
+        def project(j):
+            h, t = divmod(j, PACK)
+            junk = work.tile([P, DI], F32, name="junk", bufs=2, align_bytes=64)
+            nc.vector.scalar_tensor_tensor(out=junk[:], in0=vt[j][:], scalar=rn2[h][:, t:t + 1], in1=gs[j][:],
+                                           op0=ALU.mult, op1=ALU.mult, accum_out=gam[:, j:j + 1])
+
+        def combine(j):
+            h, t = divmod(j, PACK)
+            for a in range(2):
+                cols = slice(a * HALF, (a + 1) * HALF)
+                nc.vector.scalar_tensor_tensor(out=dv[h, a][:, t, :], in0=vt[j][:, cols], scalar=gam[:, j:j + 1],
+                                               in1=gs[j][:, cols], op0=ALU.mult, op1=ALU.subtract)
+
+        def quantize_dv(h, i0, width, il):
+            quantize(dv_codes[h][:, i0:i0 + width], dv_scales[h][:, i0:i0 + width], il[:])
+
+        g1 = {}
+        for q in range(NQ):
+            if q == 3:
+                g1[0] = interleave_g("S", 1, 0, "g1", 4)
+            xw = [widen(q, 0), widen(q, 1)]
+            gi = interleave_g("V", 0, q, "il", 3)
+            xi0 = interleave("V", xw[0][:], HALF, "il", 3)
+            if q == 3:
+                root(0)
+            quantize_g(0, q, gi)
+            xi1 = interleave("V", xw[1][:], HALF, "il", 3)
+            if q == 3:
+                alpha(0)
+            quantize_x(q, 0, xi0)
+            quantize_x(q, 1, xi1)
+            for a in range(2):
+                product(0, a, [q])
+                product(1, a, [q])
+            if q == 0:
+                gram_products(0)
+            if q == 1:
+                gram_products(1)
+            if q == 2:
+                norms(0)
+                turn_v(0)
+                turn_v(1)
+                turn_v(2)
+                recip(0)
+        g1[1] = interleave_g("S", 1, 1, "g1", 4)
+        g1[2] = interleave_g("S", 1, 2, "g1", 4)
+        norms(1)
+        turn_v(3)
+        quantize_g(1, 0, g1[0])
+        recip(1)
+        quantize_g(1, 1, g1[1])
+        scale_out(0)
+        product_tile(2)
+        project(0)
+        scale_out(1)
+        root(1)
+        product_tile(3)
+        quantize_g(1, 2, g1[2])
+        project(1)
+        alpha(1)
+        combine(0)
+        g1[3] = interleave_g("S", 1, 3, "g1", 4)
+        scale_out(2)
+        turn_v(4)
+        project(2)
+        combine(1)
+        quantize_g(1, 3, g1[3])
+        scale_out(3)
+        product_tile(4)
+        turn_v(5)
+        project(3)
+        combine(2)
+        scale_out(4)
+        product_tile(5)
+        turn_v(6)
+        combine(3)
+        project(4)
+        d0a = interleave("S", dv[0, 0][:], HALF, "g1", 4)
+        scale_out(5)
+        product_tile(6)
+        turn_v(7)
+        project(5)
+        combine(4)
+        quantize_dv(0, 0, HALF, d0a)
+        d0b = interleave("S", dv[0, 1][:], HALF, "g1", 4)
+        scale_out(6)
+        product_tile(7)
+        project(6)
+        combine(5)
+        quantize_dv(0, HALF, HALF, d0b)
+        scale_out(7)
+
+        b_words = b_sb[:].rearrange("p c o -> p (c o)").bitcast(F32)
+        b_il = work.tile([P, NH * R * PACK], BF16, name="g1", bufs=4, align_bytes=64)
+        b_il_words = b_il[:].bitcast(F32)
+        for h in range(NH):
+            bt = bank(h, "bt", [P, R // P, 2, P], F32)
+            for c in range(R // P):
+                for u in range(2):
+                    w0 = c * (DO // 2) + h * (KP // 2)
+                    nc.tensor.transpose(bt[:, c, u, :], b_words[:, w0 + u:w0 + KP // 2:2], ident_f[:])
+            nc.scalar.copy(out=b_il_words[:, h * 2 * R:(h + 1) * 2 * R].rearrange("p (c r u) -> p c r u", c=R // P, u=2),
+                           in_=bt[:].rearrange("p c u r -> p c r u"))
+        combine(6)
+        project(7)
+        quantize(b_codes[:], b_scales[:], b_il[:])
+        combine(7)
+
+        out_banks = [2, 3, 0, 1, 6, 7, 4, 5]
+
+        def second(order, c, engines):
+            res = work.tile([P, 2, R], F32, name="res", bufs=4, align_bytes=64)
+            for n in range(2):
+                i0 = c * CH + n * P
+                o_acc = bank(out_banks[2 * order + n], "oacc", [P, R], F32)
+                for h in range(NH):
+                    nc.tensor.matmul_mx(out=o_acc[:], lhsT=dv_codes[h][:, i0:i0 + P].bitcast(FP8X4),
+                                        lhsT_scale=dv_scales[h][:, i0:i0 + P],
+                                        rhs=b_codes[:, h * R:(h + 1) * R].bitcast(FP8X4),
+                                        rhs_scale=b_scales[:, h * R:(h + 1) * R],
+                                        start=(h == 0), stop=(h == NH - 1))
+                copy(engines[n], res[:, n, :], o_acc[:])
+                nc.sync.dma_start(out=out[i0:i0 + P, :], in_=res[:, n, :])
+
+        d1 = {}
+        for c in range(4):
+            d1[c] = interleave("S" if c < 2 else "V", dv[1, c // 2][:, :, (c % 2) * CH:(c % 2 + 1) * CH], CH, "d1", 4)
+        for c in (0, 2, 3, 1):
+            quantize_dv(1, c * CH, CH, d1[c])
+        second(0, 0, "SS")
+        second(1, 2, "SV")
+        second(2, 3, "SV")
+        second(3, 1, "SV")

@@ -23,6 +23,11 @@ NH = DO // KP
 HALF = 512
 NJ = NH * PACK
 CH = 256
+HEAD_V = 2
+G03 = "S"
+G13 = "V"
+G23 = "V"
+G33 = "V"
 
 
 def tile_doradirectiongradienttoloradown_kernel(tc, x_bytes, x_scale, g, v, m, b, out):
@@ -41,25 +46,26 @@ def tile_doradirectiongradienttoloradown_kernel(tc, x_bytes, x_scale, g, v, m, b
 
         xs = kept("xs", [P, NQ, PACK], F32)
         m_sb = kept("m_sb", [P, NH, PACK], BF16)
-        xb0 = [kept("xbytes0_%d" % a, [P, PACK, HALF], U8) for a in range(2)]
+        xb0 = [kept("xbytes0_%d" % a, [P, 2, DI], U8) for a in range(2)]
         xb = {q: kept("xbytes%d" % q, [P, PACK, DI], U8) for q in range(1, NQ)}
         g_raw = {(h, q): kept("graw%d_%d" % (h, q), [P, PACK, KP], BF16) for h in range(NH) for q in range(NQ)}
         v_sb = [kept("v%d" % h, [P, DI // P, KP], BF16) for h in range(NH)]
         b_sb = kept("b_sb", [P, R // P, DO], BF16)
         x_codes = [kept("xc%d" % q, [P, DI], U32) for q in range(NQ)]
         x_scales = [kept("xsc%d" % q, [P, DI], U8) for q in range(NQ)]
-        g_codes = {k: kept("gc%d_%d" % k, [P, KP], U32) for k in g_raw}
-        g_scales = {k: kept("gsc%d_%d" % k, [P, KP], U8) for k in g_raw}
+        g_codes = {(r, q): kept("gc%d_%d" % (r, q), [P, 2 * P], U32) for r in range(4) for q in range(NQ)}
+        g_scales = {(r, q): kept("gsc%d_%d" % (r, q), [P, 2 * P], U8) for r in range(4) for q in range(NQ)}
         dv_codes = [kept("dc%d" % h, [P, DI], U32) for h in range(NH)]
         dv_scales = [kept("dsc%d" % h, [P, DI], U8) for h in range(NH)]
         b_codes = kept("bc", [P, NH * R], U32)
         b_scales = kept("bsc", [P, NH * R], U8)
-        dv = {(h, a): kept("dv%d_%d" % (h, a), [P, PACK, HALF], BF16) for h in range(NH) for a in range(2)}
+        dv = [kept("dv%d" % h, [P, DI // CH, PACK, CH], BF16) for h in range(NH)]
         ident_bf = kept("ident_bf", [P, P], BF16)
         ident_f = kept("ident_f", [P, P], F32)
-        one = kept("one", [P, 1], F32)
         warm = kept("warm", [P, 1], F32)
-        n2 = [kept("n2_%d" % h, [P, PACK], F32) for h in range(NH)]
+        mask = kept("mask", [P, PACK, P // PACK], F32)
+        ones = kept("ones", [P, 2], F32)
+        masked = kept("masked", [P, PACK, P], F32)
         rn2 = [kept("rn2_%d" % h, [P, PACK], F32) for h in range(NH)]
         rn = [kept("rn_%d" % h, [P, PACK], F32) for h in range(NH)]
         nalpha = [kept("na_%d" % h, [P, PACK], F32) for h in range(NH)]
@@ -69,7 +75,7 @@ def tile_doradirectiongradienttoloradown_kernel(tc, x_bytes, x_scale, g, v, m, b
             nc.sync.dma_start(out=xb[q][:], in_=x_bytes[q * KP:(q + 1) * KP, :].rearrange("(p j) w -> p j w", j=PACK))
 
         def load_x0(a):
-            nc.sync.dma_start(out=xb0[a][:], in_=x_bytes[0:KP, a * HALF:(a + 1) * HALF].rearrange("(p j) w -> p j w", j=PACK))
+            nc.sync.dma_start(out=xb0[a][:], in_=x_bytes[0:KP, :].rearrange("(p j) w -> p j w", j=PACK)[:, 2 * a:2 * a + 2, :])
 
         def load_g(h, q):
             nc.sync.dma_start(out=g_raw[h, q][:],
@@ -78,29 +84,28 @@ def tile_doradirectiongradienttoloradown_kernel(tc, x_bytes, x_scale, g, v, m, b
         def load_v(h):
             nc.sync.dma_start(out=v_sb[h][:], in_=v[:, h * KP:(h + 1) * KP].rearrange("(a p) o -> p a o", p=P))
 
-        nc.sync.dma_start(out=xs[:], in_=x_scale.rearrange("(q p j) o -> p q (j o)", p=P, j=PACK))
+        nc.scalar.dma_start(out=xs[:], in_=x_scale.rearrange("(q p j) o -> p q (j o)", p=P, j=PACK))
         load_x0(0)
-        load_g(0, 0)
         load_x0(1)
+        load_g(0, 0)
         load_x(1)
         load_g(0, 1)
-        load_v(0)
         load_x(2)
+        load_v(0)
         load_g(0, 2)
-        load_v(1)
-        load_g(1, 0)
         load_x(3)
+        load_v(1)
         load_g(0, 3)
         nc.sync.dma_start(out=m_sb[:], in_=m.rearrange("(h p t) -> p h t", p=P, t=PACK))
-        load_g(1, 1)
-        load_g(1, 2)
-        load_g(1, 3)
+        for q in range(NQ):
+            load_g(1, q)
         nc.sync.dma_start(out=b_sb[:], in_=b.rearrange("(c p) o -> p c o", p=P))
 
-        nc.gpsimd.memset(one[:], 1.0)
-        nc.scalar.activation(out=warm[:], in_=one[:], func=ACT.Sqrt)
-        make_identity(nc, ident_bf[:])
+        nc.gpsimd.memset(ones[:], 1.0)
+        nc.scalar.activation(out=warm[:], in_=ones[:, 0:1], func=ACT.Sqrt)
         make_identity(nc, ident_f[:])
+        make_identity(nc, ident_bf[:])
+        nc.vector.tensor_copy(out=mask[:], in_=ident_f[:].rearrange("p (n t) -> p t n", t=PACK))
 
         def copy(eng, out_ap, in_ap):
             if eng == "V":
@@ -114,8 +119,12 @@ def tile_doradirectiongradienttoloradown_kernel(tc, x_bytes, x_scale, g, v, m, b
         def widen(q, a):
             xw = work.tile([P, PACK, HALF], BF16, name="xw", bufs=4, align_bytes=64)
             for j in range(PACK):
-                src = xb0[a][:, j, :] if q == 0 else xb[q][:, j, a * HALF:(a + 1) * HALF]
-                nc.scalar.activation(out=xw[:, j, :], in_=src.bitcast(FP8), func=ACT.Copy, scale=xs[:, q, j:j + 1])
+                src = (xb0[j // 2][:, j % 2] if q == 0 else xb[q][:, j])[:, a * HALF:(a + 1) * HALF]
+                if (q, a) == (0, 0) and j >= PACK - HEAD_V:
+                    nc.vector.tensor_scalar(out=xw[:, j, :], in0=src.bitcast(FP8), scalar1=xs[:, q, j:j + 1], scalar2=None,
+                                            op0=ALU.mult)
+                else:
+                    nc.scalar.activation(out=xw[:, j, :], in_=src.bitcast(FP8), func=ACT.Copy, scale=xs[:, q, j:j + 1])
             return xw
 
         def interleave(eng, planes, width, name, bufs):
@@ -124,14 +133,17 @@ def tile_doradirectiongradienttoloradown_kernel(tc, x_bytes, x_scale, g, v, m, b
                  planes.rearrange("p t (c i) -> p c t i", i=4))
             return il
 
-        def interleave_g(eng, h, q, name, bufs):
-            il = work.tile([P, KP * PACK], BF16, name=name, bufs=bufs, align_bytes=64)
-            copy(eng, il[:].rearrange("p (t c e j) -> p c j e t", t=PACK, e=2, j=PACK),
-                 g_raw[h, q][:].rearrange("p j (c e t) -> p c j e t", e=2, t=PACK))
-            return il
+        g_il = {}
 
-        def quantize_g(h, q, il):
-            quantize(g_codes[h, q][:], g_scales[h, q][:], il[:])
+        def interleave_g(eng, r, q):
+            h, u = divmod(r, 2)
+            il = work.tile([P, 2 * P * PACK], BF16, name="piece", bufs=8, align_bytes=64)
+            copy(eng, il[:].rearrange("p (t c e j) -> p c j e t", t=2, e=2, j=PACK),
+                 g_raw[h, q][:].rearrange("p j (c e u t) -> p u c j e t", e=2, u=2, t=2)[:, u])
+            g_il[r, q] = il
+
+        def quantize_g(r, q):
+            quantize(g_codes[r, q][:], g_scales[r, q][:], g_il[r, q][:])
 
         def quantize_x(q, a, il):
             cols = slice(a * HALF, (a + 1) * HALF)
@@ -140,13 +152,13 @@ def tile_doradirectiongradienttoloradown_kernel(tc, x_bytes, x_scale, g, v, m, b
         acc = {}
 
         def product(j, a, passes):
-            h, t = divmod(j, PACK)
+            r, t = divmod(j, 2)
             if (j, a) not in acc:
                 acc[j, a] = bank(2 * (j % 2) + a, "acc", [P, HALF], F32)
             oc = slice(t * P, (t + 1) * P)
             ic = slice(a * HALF, (a + 1) * HALF)
             for q in passes:
-                nc.tensor.matmul_mx(out=acc[j, a][:], lhsT=g_codes[h, q][:, oc].bitcast(FP8X4), lhsT_scale=g_scales[h, q][:, oc],
+                nc.tensor.matmul_mx(out=acc[j, a][:], lhsT=g_codes[r, q][:, oc].bitcast(FP8X4), lhsT_scale=g_scales[r, q][:, oc],
                                     rhs=x_codes[q][:, ic].bitcast(FP8X4), rhs_scale=x_scales[q][:, ic],
                                     start=(q == 0), stop=(q == NQ - 1))
 
@@ -160,17 +172,23 @@ def tile_doradirectiongradienttoloradown_kernel(tc, x_bytes, x_scale, g, v, m, b
             gram[h] = bank(4 + h, "gram", [P, PACK, P], F32)
             for t in range(PACK):
                 for c in range(DI // P):
-                    cols = v_sb[h][:, c, t:KP:PACK]
+                    cols = v_sb[h][:, c, t * P:(t + 1) * P]
                     nc.tensor.matmul(out=gram[h][:, t, :], lhsT=cols, rhs=cols, start=(c == 0), stop=(c == DI // P - 1))
 
-        def norms(h):
+        def mask_gram(h):
+            nc.vector.tensor_tensor(out=masked[:].rearrange("p t (c n) -> p t c n", c=PACK),
+                                    in0=gram[h][:].rearrange("p c (n t) -> p t c n", t=PACK),
+                                    in1=mask[:].unsqueeze(2).broadcast_to([P, PACK, PACK, P // PACK]), op=ALU.mult)
+
+        n2 = {}
+
+        def column_sums(h):
+            n2[h] = bank(4 + h, "n2", [P, PACK, 2], F32)
             for t in range(PACK):
-                junk = work.tile([P, DI], F32, name="junk", bufs=2, align_bytes=64)
-                nc.vector.scalar_tensor_tensor(out=junk[:, 0:P], in0=gram[h][:, t, :], scalar=1.0, in1=ident_f[:],
-                                               op0=ALU.mult, op1=ALU.mult, accum_out=n2[h][:, t:t + 1])
+                nc.tensor.matmul(out=n2[h][:, t, :], lhsT=masked[:, t, :], rhs=ones[:], start=True, stop=True)
 
         def recip(h):
-            nc.vector.reciprocal(out=rn2[h][:], in_=n2[h][:])
+            nc.vector.reciprocal(out=rn2[h][:], in_=n2[h][:, :, 0])
 
         def root(h):
             nc.scalar.activation(out=rn[h][:], in_=rn2[h][:], func=ACT.Sqrt)
@@ -191,7 +209,7 @@ def tile_doradirectiongradienttoloradown_kernel(tc, x_bytes, x_scale, g, v, m, b
 
         def scale_out(j):
             h, t = divmod(j, PACK)
-            gs[j] = work.tile([P, DI], F32, name="gs", bufs=4, align_bytes=64)
+            gs[j] = work.tile([P, DI], F32, name="gs", bufs=5, align_bytes=64)
             for a in range(2):
                 nc.scalar.activation(out=gs[j][:, a * HALF:(a + 1) * HALF], in_=acc[j, a][:], func=ACT.Copy,
                                      scale=nalpha[h][:, t:t + 1])
@@ -202,30 +220,44 @@ def tile_doradirectiongradienttoloradown_kernel(tc, x_bytes, x_scale, g, v, m, b
             nc.vector.scalar_tensor_tensor(out=junk[:], in0=vt[j][:], scalar=rn2[h][:, t:t + 1], in1=gs[j][:],
                                            op0=ALU.mult, op1=ALU.mult, accum_out=gam[:, j:j + 1])
 
-        def combine(j):
+        def combine(j, c0=0, c1=DI // CH):
             h, t = divmod(j, PACK)
-            for a in range(2):
-                cols = slice(a * HALF, (a + 1) * HALF)
-                nc.vector.scalar_tensor_tensor(out=dv[h, a][:, t, :], in0=vt[j][:, cols], scalar=gam[:, j:j + 1],
-                                               in1=gs[j][:, cols], op0=ALU.mult, op1=ALU.subtract)
+            cols = slice(c0 * CH, c1 * CH)
+            nc.vector.scalar_tensor_tensor(out=dv[h][:, c0:c1, t, :], in0=vt[j][:, cols].rearrange("p (c i) -> p c i", i=CH),
+                                           scalar=gam[:, j:j + 1], in1=gs[j][:, cols].rearrange("p (c i) -> p c i", i=CH),
+                                           op0=ALU.mult, op1=ALU.subtract)
 
         def quantize_dv(h, i0, width, il):
             quantize(dv_codes[h][:, i0:i0 + width], dv_scales[h][:, i0:i0 + width], il[:])
 
-        g1 = {}
+        dv_il = {}
+
+        def interleave_dv(eng, h, c):
+            dv_il[h, c] = interleave(eng, dv[h][:, c], CH, "piece", 8)
+
+        def quantize_dv_piece(h, c):
+            quantize_dv(h, c * CH, CH, dv_il[h, c])
+
         for q in range(NQ):
-            if q == 3:
-                g1[0] = interleave_g("S", 1, 0, "g1", 4)
             xw = [widen(q, 0), widen(q, 1)]
-            gi = interleave_g("V", 0, q, "il", 3)
             xi0 = interleave("V", xw[0][:], HALF, "il", 3)
             if q == 3:
                 root(0)
-            quantize_g(0, q, gi)
-            xi1 = interleave("V", xw[1][:], HALF, "il", 3)
+            interleave_g(G03 if q == 3 else "V", 0, q)
+            if q == 3:
+                mask_gram(1)
+                column_sums(1)
+            quantize_x(q, 0, xi0)
+            if q == 2:
+                mask_gram(0)
+                column_sums(0)
+                gram_products(1)
             if q == 3:
                 alpha(0)
-            quantize_x(q, 0, xi0)
+            xi1 = interleave("V", xw[1][:], HALF, "il", 3)
+            quantize_g(0, q)
+            if q == 2:
+                recip(0)
             quantize_x(q, 1, xi1)
             for a in range(2):
                 product(0, a, [q])
@@ -233,63 +265,73 @@ def tile_doradirectiongradienttoloradown_kernel(tc, x_bytes, x_scale, g, v, m, b
             if q == 0:
                 gram_products(0)
             if q == 1:
-                gram_products(1)
-            if q == 2:
-                norms(0)
                 turn_v(0)
+            if q == 2:
                 turn_v(1)
-                turn_v(2)
-                recip(0)
-        g1[1] = interleave_g("S", 1, 1, "g1", 4)
-        g1[2] = interleave_g("S", 1, 2, "g1", 4)
-        norms(1)
-        turn_v(3)
-        quantize_g(1, 0, g1[0])
+        for q in range(3):
+            interleave_g("S", 1, q)
         recip(1)
-        quantize_g(1, 1, g1[1])
+        turn_v(2)
+        turn_v(3)
+        interleave_g(G13, 1, 3)
+        for q in range(NQ):
+            quantize_g(1, q)
         scale_out(0)
-        product_tile(2)
-        project(0)
         scale_out(1)
         root(1)
+        product_tile(2)
+
         product_tile(3)
-        quantize_g(1, 2, g1[2])
-        project(1)
+
+        for q in range(3):
+            interleave_g("S", 2, q)
+        project(0)
+        interleave_g(G23, 2, 3)
         alpha(1)
         combine(0)
-        g1[3] = interleave_g("S", 1, 3, "g1", 4)
         scale_out(2)
-        turn_v(4)
-        project(2)
-        combine(1)
-        quantize_g(1, 3, g1[3])
         scale_out(3)
+        project(1)
+        for q in (3, 0, 1, 2):
+            quantize_g(2, q)
+        turn_v(4)
         product_tile(4)
+        product_tile(5)
+        combine(1)
         turn_v(5)
-        project(3)
+        for q in range(3):
+            interleave_g("S", 3, q)
+        project(2)
+        interleave_g(G33, 3, 3)
         combine(2)
         scale_out(4)
-        product_tile(5)
-        turn_v(6)
-        combine(3)
-        project(4)
-        d0a = interleave("S", dv[0, 0][:], HALF, "g1", 4)
         scale_out(5)
+        project(3)
+        for q in (3, 0, 1, 2):
+            quantize_g(3, q)
         product_tile(6)
-        turn_v(7)
-        project(5)
-        combine(4)
-        quantize_dv(0, 0, HALF, d0a)
-        d0b = interleave("S", dv[0, 1][:], HALF, "g1", 4)
-        scale_out(6)
+        turn_v(6)
         product_tile(7)
-        project(6)
+        combine(3)
+        turn_v(7)
+        project(4)
+        combine(4)
+        interleave_dv("S", 0, 0)
+        interleave_dv("S", 0, 1)
+        project(5)
+        quantize_dv_piece(0, 0)
         combine(5)
-        quantize_dv(0, HALF, HALF, d0b)
+        scale_out(6)
+        interleave_dv("S", 0, 2)
+        interleave_dv("S", 0, 3)
+        project(6)
+        quantize_dv_piece(0, 1)
+        quantize_dv_piece(0, 2)
+        combine(6)
         scale_out(7)
 
         b_words = b_sb[:].rearrange("p c o -> p (c o)").bitcast(F32)
-        b_il = work.tile([P, NH * R * PACK], BF16, name="g1", bufs=4, align_bytes=64)
+        b_il = work.tile([P, NH * R * PACK], BF16, name="il", bufs=3, align_bytes=64)
         b_il_words = b_il[:].bitcast(F32)
         for h in range(NH):
             bt = bank(h, "bt", [P, R // P, 2, P], F32)
@@ -299,33 +341,44 @@ def tile_doradirectiongradienttoloradown_kernel(tc, x_bytes, x_scale, g, v, m, b
                     nc.tensor.transpose(bt[:, c, u, :], b_words[:, w0 + u:w0 + KP // 2:2], ident_f[:])
             nc.scalar.copy(out=b_il_words[:, h * 2 * R:(h + 1) * 2 * R].rearrange("p (c r u) -> p c r u", c=R // P, u=2),
                            in_=bt[:].rearrange("p c u r -> p c r u"))
-        combine(6)
+        quantize_dv_piece(0, 3)
         project(7)
         quantize(b_codes[:], b_scales[:], b_il[:])
-        combine(7)
+        for c in range(DI // CH):
+            combine(7, c, c + 1)
 
         out_banks = [2, 3, 0, 1, 6, 7, 4, 5]
+        o_acc = {}
 
-        def second(order, c, engines):
-            res = work.tile([P, 2, R], F32, name="res", bufs=4, align_bytes=64)
-            for n in range(2):
-                i0 = c * CH + n * P
-                o_acc = bank(out_banks[2 * order + n], "oacc", [P, R], F32)
-                for h in range(NH):
-                    nc.tensor.matmul_mx(out=o_acc[:], lhsT=dv_codes[h][:, i0:i0 + P].bitcast(FP8X4),
-                                        lhsT_scale=dv_scales[h][:, i0:i0 + P],
-                                        rhs=b_codes[:, h * R:(h + 1) * R].bitcast(FP8X4),
-                                        rhs_scale=b_scales[:, h * R:(h + 1) * R],
-                                        start=(h == 0), stop=(h == NH - 1))
-                copy(engines[n], res[:, n, :], o_acc[:])
-                nc.sync.dma_start(out=out[i0:i0 + P, :], in_=res[:, n, :])
+        def second(n, h):
+            i0 = n * P
+            if h == 0:
+                o_acc[n] = bank(out_banks[n], "oacc", [P, R], F32)
+            nc.tensor.matmul_mx(out=o_acc[n][:], lhsT=dv_codes[h][:, i0:i0 + P].bitcast(FP8X4),
+                                lhsT_scale=dv_scales[h][:, i0:i0 + P],
+                                rhs=b_codes[:, h * R:(h + 1) * R].bitcast(FP8X4),
+                                rhs_scale=b_scales[:, h * R:(h + 1) * R],
+                                start=(h == 0), stop=(h == NH - 1))
 
-        d1 = {}
-        for c in range(4):
-            d1[c] = interleave("S" if c < 2 else "V", dv[1, c // 2][:, :, (c % 2) * CH:(c % 2 + 1) * CH], CH, "d1", 4)
-        for c in (0, 2, 3, 1):
-            quantize_dv(1, c * CH, CH, d1[c])
-        second(0, 0, "SS")
-        second(1, 2, "SV")
-        second(2, 3, "SV")
-        second(3, 1, "SV")
+        def finish(c, engines):
+            for k in range(2):
+                n = 2 * c + k
+                second(n, 1)
+                res = work.tile([P, R], F32, name="res", bufs=8, align_bytes=64)
+                copy(engines[k], res[:], o_acc[n][:])
+                nc.sync.dma_start(out=out[n * P:(n + 1) * P, :], in_=res[:])
+
+        for n in range(DI // P):
+            second(n, 0)
+        interleave_dv("S", 1, 0)
+        interleave_dv("S", 1, 1)
+        interleave_dv("V", 1, 2)
+        quantize_dv_piece(1, 0)
+        quantize_dv_piece(1, 2)
+        interleave_dv("V", 1, 3)
+        quantize_dv_piece(1, 1)
+        quantize_dv_piece(1, 3)
+        finish(0, "SS")
+        finish(2, "SS")
+        finish(1, "SV")
+        finish(3, "SV")

@@ -23,7 +23,8 @@ NH = DO // KP
 HALF = 512
 NJ = NH * PACK
 CH = 256
-HEAD_V = 2
+HEAD_V = 4
+LATE = (1, 0, 0)
 G03 = "S"
 G13 = "V"
 G23 = "V"
@@ -46,7 +47,7 @@ def tile_doradirectiongradienttoloradown_kernel(tc, x_bytes, x_scale, g, v, m, b
 
         xs = kept("xs", [P, NQ, PACK], F32)
         m_sb = kept("m_sb", [P, NH, PACK], BF16)
-        xb0 = [kept("xbytes0_%d" % a, [P, 2, DI], U8) for a in range(2)]
+        xb0 = [kept("xbytes0_%d" % a, [P, DI], U8) for a in range(PACK)]
         xb = {q: kept("xbytes%d" % q, [P, PACK, DI], U8) for q in range(1, NQ)}
         g_raw = {(h, q): kept("graw%d_%d" % (h, q), [P, PACK, KP], BF16) for h in range(NH) for q in range(NQ)}
         v_sb = [kept("v%d" % h, [P, DI // P, KP], BF16) for h in range(NH)]
@@ -60,7 +61,6 @@ def tile_doradirectiongradienttoloradown_kernel(tc, x_bytes, x_scale, g, v, m, b
         b_codes = kept("bc", [P, NH * R], U32)
         b_scales = kept("bsc", [P, NH * R], U8)
         dv = [kept("dv%d" % h, [P, DI // CH, PACK, CH], BF16) for h in range(NH)]
-        ident_bf = kept("ident_bf", [P, P], BF16)
         ident_f = kept("ident_f", [P, P], F32)
         warm = kept("warm", [P, 1], F32)
         mask = kept("mask", [P, PACK, P // PACK], F32)
@@ -70,12 +70,13 @@ def tile_doradirectiongradienttoloradown_kernel(tc, x_bytes, x_scale, g, v, m, b
         rn = [kept("rn_%d" % h, [P, PACK], F32) for h in range(NH)]
         nalpha = [kept("na_%d" % h, [P, PACK], F32) for h in range(NH)]
         gam = kept("gam", [P, NJ], F32)
+        part = kept("part", [P, NJ, 2], F32)
 
         def load_x(q):
             nc.sync.dma_start(out=xb[q][:], in_=x_bytes[q * KP:(q + 1) * KP, :].rearrange("(p j) w -> p j w", j=PACK))
 
         def load_x0(a):
-            nc.sync.dma_start(out=xb0[a][:], in_=x_bytes[0:KP, :].rearrange("(p j) w -> p j w", j=PACK)[:, 2 * a:2 * a + 2, :])
+            nc.sync.dma_start(out=xb0[a][:], in_=x_bytes[0:KP, :].rearrange("(p j) w -> p j w", j=PACK)[:, a, :])
 
         def load_g(h, q):
             nc.sync.dma_start(out=g_raw[h, q][:],
@@ -85,17 +86,17 @@ def tile_doradirectiongradienttoloradown_kernel(tc, x_bytes, x_scale, g, v, m, b
             nc.sync.dma_start(out=v_sb[h][:], in_=v[:, h * KP:(h + 1) * KP].rearrange("(a p) o -> p a o", p=P))
 
         nc.scalar.dma_start(out=xs[:], in_=x_scale.rearrange("(q p j) o -> p q (j o)", p=P, j=PACK))
-        load_x0(0)
-        load_x0(1)
-        load_g(0, 0)
+        for j in range(PACK):
+            load_x0(j)
         load_x(1)
-        load_g(0, 1)
+        load_g(0, 0)
         load_x(2)
+        load_g(0, 1)
         load_v(0)
-        load_g(0, 2)
         load_x(3)
-        load_v(1)
+        load_g(0, 2)
         load_g(0, 3)
+        load_v(1)
         nc.sync.dma_start(out=m_sb[:], in_=m.rearrange("(h p t) -> p h t", p=P, t=PACK))
         for q in range(NQ):
             load_g(1, q)
@@ -104,12 +105,13 @@ def tile_doradirectiongradienttoloradown_kernel(tc, x_bytes, x_scale, g, v, m, b
         nc.gpsimd.memset(ones[:], 1.0)
         nc.scalar.activation(out=warm[:], in_=ones[:, 0:1], func=ACT.Sqrt)
         make_identity(nc, ident_f[:])
-        make_identity(nc, ident_bf[:])
         nc.vector.tensor_copy(out=mask[:], in_=ident_f[:].rearrange("p (n t) -> p t n", t=PACK))
 
         def copy(eng, out_ap, in_ap):
             if eng == "V":
                 nc.vector.tensor_copy(out=out_ap, in_=in_ap)
+            elif eng == "G":
+                nc.gpsimd.tensor_scalar(out=out_ap, in0=in_ap, scalar1=1.0, scalar2=0.0, op0=ALU.mult, op1=ALU.add)
             else:
                 nc.scalar.copy(out=out_ap, in_=in_ap)
 
@@ -119,7 +121,7 @@ def tile_doradirectiongradienttoloradown_kernel(tc, x_bytes, x_scale, g, v, m, b
         def widen(q, a):
             xw = work.tile([P, PACK, HALF], BF16, name="xw", bufs=4, align_bytes=64)
             for j in range(PACK):
-                src = (xb0[j // 2][:, j % 2] if q == 0 else xb[q][:, j])[:, a * HALF:(a + 1) * HALF]
+                src = (xb0[j][:] if q == 0 else xb[q][:, j])[:, a * HALF:(a + 1) * HALF]
                 if (q, a) == (0, 0) and j >= PACK - HEAD_V:
                     nc.vector.tensor_scalar(out=xw[:, j, :], in0=src.bitcast(FP8), scalar1=xs[:, q, j:j + 1], scalar2=None,
                                             op0=ALU.mult)
@@ -129,17 +131,25 @@ def tile_doradirectiongradienttoloradown_kernel(tc, x_bytes, x_scale, g, v, m, b
 
         def interleave(eng, planes, width, name, bufs):
             il = work.tile([P, width * PACK], BF16, name=name, bufs=bufs, align_bytes=64)
-            copy(eng, il[:].rearrange("p (c i t) -> p c t i", i=4, t=PACK),
-                 planes.rearrange("p t (c i) -> p c t i", i=4))
+            if eng == "G":
+                copy(eng, il[:].rearrange("p (c t) -> p c t", t=PACK), planes.rearrange("p t c -> p c t"))
+            else:
+                copy(eng, il[:].rearrange("p (c i t) -> p c t i", i=4, t=PACK),
+                     planes.rearrange("p t (c i) -> p c t i", i=4))
             return il
 
         g_il = {}
 
-        def interleave_g(eng, r, q):
+        def interleave_g(eng, r, q, gate=False):
             h, u = divmod(r, 2)
-            il = work.tile([P, 2 * P * PACK], BF16, name="piece", bufs=8, align_bytes=64)
-            copy(eng, il[:].rearrange("p (t c e j) -> p c j e t", t=2, e=2, j=PACK),
-                 g_raw[h, q][:].rearrange("p j (c e u t) -> p u c j e t", e=2, u=2, t=2)[:, u])
+            if eng == "G":
+                il = work.tile([P, 2 * P * PACK], BF16, name="gate", bufs=1, align_bytes=64)
+                copy(eng, il[:].rearrange("p (t c j) -> p t c j", t=2, j=PACK),
+                     g_raw[h, q][:].rearrange("p j (c u t) -> p u t c j", u=2, t=2)[:, u])
+            else:
+                il = work.tile([P, 2 * P * PACK], BF16, name="gate" if gate else "piece", bufs=1 if gate else 8, align_bytes=64)
+                copy(eng, il[:].rearrange("p (t c e j) -> p c j e t", t=2, e=2, j=PACK),
+                     g_raw[h, q][:].rearrange("p j (c e u t) -> p u c j e t", e=2, u=2, t=2)[:, u])
             g_il[r, q] = il
 
         def quantize_g(r, q):
@@ -199,33 +209,97 @@ def tile_doradirectiongradienttoloradown_kernel(tc, x_bytes, x_scale, g, v, m, b
 
         vt = {}
 
-        def turn_v(j):
-            h, t = divmod(j, PACK)
-            vt[j] = bank(4 + (j + 2) % 4, "vt", [P, DI], BF16)
-            for c in range(DI // P):
-                nc.tensor.transpose(vt[j][:, c * P:(c + 1) * P], v_sb[h][:, c, t:KP:PACK], ident_bf[:])
+        def turn_v(r):
+            h, u = divmod(r, 2)
+            words = v_sb[h][:].rearrange("p c o -> p (c o)").bitcast(F32)
+            for a in range(2):
+                vt[r, a] = bank(4 + 2 * ((r + 1) % 2) + a, "vt", [P, HALF], F32)
+                for c in range(HALF // P):
+                    w0 = (a * (HALF // P) + c) * (KP // 2)
+                    nc.tensor.transpose(vt[r, a][:, c * P:(c + 1) * P], words[:, w0 + u:w0 + KP // 2:2], ident_f[:])
+
+        def v_t(j, a):
+            return vt[j // 2, a][:].bitcast(BF16)[:, j % 2:2 * HALF:2]
 
         gs = {}
 
-        def scale_out(j):
+        def scale_out(j, a):
             h, t = divmod(j, PACK)
-            gs[j] = work.tile([P, DI], F32, name="gs", bufs=5, align_bytes=64)
-            for a in range(2):
-                nc.scalar.activation(out=gs[j][:, a * HALF:(a + 1) * HALF], in_=acc[j, a][:], func=ACT.Copy,
-                                     scale=nalpha[h][:, t:t + 1])
+            if a == 0:
+                gs[j] = work.tile([P, DI], F32, name="gs", bufs=5, align_bytes=64)
+            nc.scalar.activation(out=gs[j][:, a * HALF:(a + 1) * HALF], in_=acc[j, a][:], func=ACT.Copy,
+                                 scale=nalpha[h][:, t:t + 1])
 
-        def project(j):
+        def project(j, a):
             h, t = divmod(j, PACK)
-            junk = work.tile([P, DI], F32, name="junk", bufs=2, align_bytes=64)
-            nc.vector.scalar_tensor_tensor(out=junk[:], in0=vt[j][:], scalar=rn2[h][:, t:t + 1], in1=gs[j][:],
-                                           op0=ALU.mult, op1=ALU.mult, accum_out=gam[:, j:j + 1])
+            junk = work.tile([P, HALF], F32, name="junk", bufs=2, align_bytes=64)
+            nc.vector.scalar_tensor_tensor(out=junk[:], in0=v_t(j, a), scalar=rn2[h][:, t:t + 1],
+                                           in1=gs[j][:, a * HALF:(a + 1) * HALF],
+                                           op0=ALU.mult, op1=ALU.mult, accum_out=part[:, j, a:a + 1])
 
-        def combine(j, c0=0, c1=DI // CH):
+        def join(r):
+            j = slice(2 * r, 2 * r + 2)
+            nc.vector.tensor_tensor(out=gam[:, j], in0=part[:, j, 0], in1=part[:, j, 1], op=ALU.add)
+
+        def combine(j, c0, c1):
             h, t = divmod(j, PACK)
-            cols = slice(c0 * CH, c1 * CH)
-            nc.vector.scalar_tensor_tensor(out=dv[h][:, c0:c1, t, :], in0=vt[j][:, cols].rearrange("p (c i) -> p c i", i=CH),
-                                           scalar=gam[:, j:j + 1], in1=gs[j][:, cols].rearrange("p (c i) -> p c i", i=CH),
+            a = c0 // 2
+            nc.vector.scalar_tensor_tensor(out=dv[h][:, c0:c1, t, :],
+                                           in0=v_t(j, a)[:, (c0 - 2 * a) * CH:(c1 - 2 * a) * CH].rearrange("p (c i) -> p c i", i=CH),
+                                           scalar=gam[:, j:j + 1],
+                                           in1=gs[j][:, c0 * CH:c1 * CH].rearrange("p (c i) -> p c i", i=CH),
                                            op0=ALU.mult, op1=ALU.subtract)
+
+        def projections(r):
+            j = 2 * r
+            project(j, 0)
+            project(j + 1, 0)
+            project(j, 1)
+            project(j + 1, 1)
+            join(r)
+
+        def combinations(r):
+            for j in (2 * r, 2 * r + 1):
+                combine(j, 0, 2)
+                combine(j, 2, 4)
+
+        def pair(r, jobs, last=False):
+            j = 2 * r
+            project(j, 0)
+            project(j, 1)
+            project(j + 1, 0)
+            join1(j)
+            project(j + 1, 1)
+            if last:
+                jobs()
+                join1(j + 1)
+            else:
+                combine(j, 0, 2)
+                join1(j + 1)
+                if LATE[r]:
+                    combine(j, 2, 4)
+                    jobs()
+                else:
+                    jobs()
+                    combine(j, 2, 4)
+                combine(j + 1, 0, 2)
+                combine(j + 1, 2, 4)
+
+        def join1(j):
+            nc.vector.tensor_tensor(out=gam[:, j:j + 1], in0=part[:, j, 0:1], in1=part[:, j, 1:2], op=ALU.add)
+
+        def scale_tile(j):
+            scale_out(j, 0)
+            scale_out(j, 1)
+
+        def products(r):
+            for a in range(2):
+                product(2 * r, a, range(NQ))
+                product(2 * r + 1, a, range(NQ))
+
+        def scale_half(r, a):
+            scale_out(2 * r, a)
+            scale_out(2 * r + 1, a)
 
         def quantize_dv(h, i0, width, il):
             quantize(dv_codes[h][:, i0:i0 + width], dv_scales[h][:, i0:i0 + width], il[:])
@@ -233,32 +307,53 @@ def tile_doradirectiongradienttoloradown_kernel(tc, x_bytes, x_scale, g, v, m, b
         dv_il = {}
 
         def interleave_dv(eng, h, c):
-            dv_il[h, c] = interleave(eng, dv[h][:, c], CH, "piece", 8)
+            dv_il[h, c] = interleave(eng, dv[h][:, c], CH, *(("gate", 1) if eng == "G" else ("piece", 8)))
 
         def quantize_dv_piece(h, c):
             quantize_dv(h, c * CH, CH, dv_il[h, c])
 
+        def turn_b():
+            b_words = b_sb[:].rearrange("p c o -> p (c o)").bitcast(F32)
+            b_il = work.tile([P, NH * R * PACK], BF16, name="il", bufs=3, align_bytes=64)
+            b_il_words = b_il[:].bitcast(F32)
+            for h in range(NH):
+                bt = bank(h, "bt", [P, R // P, 2, P], F32)
+                for c in range(R // P):
+                    for u in range(2):
+                        w0 = c * (DO // 2) + h * (KP // 2)
+                        nc.tensor.transpose(bt[:, c, u, :], b_words[:, w0 + u:w0 + KP // 2:2], ident_f[:])
+                nc.scalar.copy(out=b_il_words[:, h * 2 * R:(h + 1) * 2 * R].rearrange("p (c r u) -> p c r u", c=R // P, u=2),
+                               in_=bt[:].rearrange("p c u r -> p c r u"))
+            return b_il
+
         for q in range(NQ):
             xw = [widen(q, 0), widen(q, 1)]
             xi0 = interleave("V", xw[0][:], HALF, "il", 3)
+            if q == 0:
+                xi1 = interleave("V", xw[1][:], HALF, "il", 3)
+                quantize_x(q, 0, xi0)
+                interleave_g("V", 0, q)
+                quantize_x(q, 1, xi1)
+                quantize_g(0, q)
+                for a in range(2):
+                    product(0, a, [q])
+                    product(1, a, [q])
+                gram_products(0)
+                continue
+            interleave_g("S" if q == 3 else "V", 0, q)
             if q == 3:
                 root(0)
-            interleave_g(G03 if q == 3 else "V", 0, q)
-            if q == 3:
-                mask_gram(1)
-                column_sums(1)
             quantize_x(q, 0, xi0)
             if q == 2:
                 mask_gram(0)
                 column_sums(0)
-                gram_products(1)
-            if q == 3:
-                alpha(0)
             xi1 = interleave("V", xw[1][:], HALF, "il", 3)
             quantize_g(0, q)
+            if q == 3:
+                alpha(0)
+            quantize_x(q, 1, xi1)
             if q == 2:
                 recip(0)
-            quantize_x(q, 1, xi1)
             for a in range(2):
                 product(0, a, [q])
                 product(1, a, [q])
@@ -267,87 +362,75 @@ def tile_doradirectiongradienttoloradown_kernel(tc, x_bytes, x_scale, g, v, m, b
             if q == 1:
                 turn_v(0)
             if q == 2:
-                turn_v(1)
+                gram_products(1)
         for q in range(3):
             interleave_g("S", 1, q)
-        recip(1)
-        turn_v(2)
-        turn_v(3)
-        interleave_g(G13, 1, 3)
+        mask_gram(1)
+        column_sums(1)
+        interleave_g("S", 1, 3, True)
         for q in range(NQ):
             quantize_g(1, q)
-        scale_out(0)
-        scale_out(1)
+        scale_tile(0)
+        scale_tile(1)
+        recip(1)
         root(1)
         product_tile(2)
-
+        turn_v(1)
         product_tile(3)
-
+        interleave_g("V", 2, 3)
         for q in range(3):
             interleave_g("S", 2, q)
-        project(0)
-        interleave_g(G23, 2, 3)
-        alpha(1)
-        combine(0)
-        scale_out(2)
-        scale_out(3)
-        project(1)
-        for q in (3, 0, 1, 2):
-            quantize_g(2, q)
-        turn_v(4)
+
+        def jobs0():
+            alpha(1)
+            for q in (0, 1, 2, 3):
+                quantize_g(2, q)
+
+        scale_tile(2)
+        scale_tile(3)
+        pair(0, jobs0)
         product_tile(4)
+        turn_v(2)
         product_tile(5)
-        combine(1)
-        turn_v(5)
+        interleave_g("V", 3, 3)
         for q in range(3):
             interleave_g("S", 3, q)
-        project(2)
-        interleave_g(G33, 3, 3)
-        combine(2)
-        scale_out(4)
-        scale_out(5)
-        project(3)
-        for q in (3, 0, 1, 2):
-            quantize_g(3, q)
+
+        def jobs1():
+            for q in (0, 1, 2, 3):
+                quantize_g(3, q)
+
+        pair(1, jobs1)
+        scale_tile(4)
+        scale_tile(5)
         product_tile(6)
-        turn_v(6)
+        turn_v(3)
         product_tile(7)
-        combine(3)
-        turn_v(7)
-        project(4)
-        combine(4)
         interleave_dv("S", 0, 0)
         interleave_dv("S", 0, 1)
-        project(5)
-        quantize_dv_piece(0, 0)
-        combine(5)
-        scale_out(6)
+        scale_tile(6)
         interleave_dv("S", 0, 2)
-        interleave_dv("S", 0, 3)
-        project(6)
-        quantize_dv_piece(0, 1)
-        quantize_dv_piece(0, 2)
-        combine(6)
-        scale_out(7)
 
-        b_words = b_sb[:].rearrange("p c o -> p (c o)").bitcast(F32)
-        b_il = work.tile([P, NH * R * PACK], BF16, name="il", bufs=3, align_bytes=64)
-        b_il_words = b_il[:].bitcast(F32)
-        for h in range(NH):
-            bt = bank(h, "bt", [P, R // P, 2, P], F32)
-            for c in range(R // P):
-                for u in range(2):
-                    w0 = c * (DO // 2) + h * (KP // 2)
-                    nc.tensor.transpose(bt[:, c, u, :], b_words[:, w0 + u:w0 + KP // 2:2], ident_f[:])
-            nc.scalar.copy(out=b_il_words[:, h * 2 * R:(h + 1) * 2 * R].rearrange("p (c r u) -> p c r u", c=R // P, u=2),
-                           in_=bt[:].rearrange("p c u r -> p c r u"))
-        quantize_dv_piece(0, 3)
-        project(7)
-        quantize(b_codes[:], b_scales[:], b_il[:])
+        def jobs2():
+            quantize_dv_piece(0, 1)
+            quantize_dv_piece(0, 0)
+
+        pair(2, jobs2)
+        scale_tile(7)
+        interleave_dv("S", 0, 3)
+        b_il = turn_b()
+
+        def jobs3():
+            quantize_dv_piece(0, 2)
+            quantize_dv_piece(0, 3)
+            quantize(b_codes[:], b_scales[:], b_il[:])
+
+        pair(3, jobs3, True)
         for c in range(DI // CH):
+            combine(6, c, c + 1)
             combine(7, c, c + 1)
 
-        out_banks = [2, 3, 0, 1, 6, 7, 4, 5]
+        out_banks = [6, 7, 0, 1, 2, 3, 4, 5]
         o_acc = {}
 
         def second(n, h):
@@ -372,13 +455,13 @@ def tile_doradirectiongradienttoloradown_kernel(tc, x_bytes, x_scale, g, v, m, b
             second(n, 0)
         interleave_dv("S", 1, 0)
         interleave_dv("S", 1, 1)
-        interleave_dv("V", 1, 2)
+        interleave_dv("S", 1, 2)
         quantize_dv_piece(1, 0)
-        quantize_dv_piece(1, 2)
         interleave_dv("V", 1, 3)
         quantize_dv_piece(1, 1)
+        finish(0, "VV")
         quantize_dv_piece(1, 3)
-        finish(0, "SS")
-        finish(2, "SS")
-        finish(1, "SV")
+        quantize_dv_piece(1, 2)
+        finish(1, "SS")
         finish(3, "SV")
+        finish(2, "SV")

@@ -17,18 +17,23 @@ ALU = mybir.AluOpType
 
 P = 128
 PACK = 4
-KP = P * PACK
-NQ = T // KP
-NH = DO // KP
-HALF = 512
-NJ = NH * PACK
-CH = 256
-HEAD_V = 4
-LATE = (1, 0, 0)
-G03 = "S"
-G13 = "V"
-G23 = "V"
-G33 = "V"
+K_PASS = P * PACK
+TOKEN_PASSES = T // K_PASS
+COLUMN_PASSES = DO // K_PASS
+TILES = COLUMN_PASSES * PACK
+PAIRS = TILES // 2
+HALF = DI // 2
+QUARTER = DI // 4
+ROW_TILES = DI // P
+RUN = 4
+LAST = TOKEN_PASSES - 1
+
+WIDENED_SLOTS = 4
+WIDE_SLOTS = 3
+PIECE_SLOTS = 8
+SCALED_SLOTS = 5
+OUT_BANKS = (6, 7, 0, 1, 2, 3, 4, 5)
+EARLY_OUT_TILES = 6
 
 
 def tile_doradirectiongradienttoloradown_kernel(tc, x_bytes, x_scale, g, v, m, b, out):
@@ -42,52 +47,61 @@ def tile_doradirectiongradienttoloradown_kernel(tc, x_bytes, x_scale, g, v, m, b
         def kept(name, shape, dtype):
             return keep.tile(shape, dtype, name=name, align_bytes=64)
 
-        def bank(k, name, shape, dtype):
-            return psum.tile(shape, dtype, name=name, tag="bank%d" % k)
+        def rotating(name, slots, shape, dtype):
+            return work.tile(shape, dtype, name=name, bufs=slots, align_bytes=64)
 
-        xs = kept("xs", [P, NQ, PACK], F32)
-        m_sb = kept("m_sb", [P, NH, PACK], BF16)
-        xb0 = [kept("xbytes0_%d" % a, [P, DI], U8) for a in range(PACK)]
-        xb = {q: kept("xbytes%d" % q, [P, PACK, DI], U8) for q in range(1, NQ)}
-        g_raw = {(h, q): kept("graw%d_%d" % (h, q), [P, PACK, KP], BF16) for h in range(NH) for q in range(NQ)}
-        v_sb = [kept("v%d" % h, [P, DI // P, KP], BF16) for h in range(NH)]
+        def bank(number, name, shape, dtype):
+            return psum.tile(shape, dtype, name=name, tag="bank%d" % number)
+
+        def half(a):
+            return slice(a * HALF, (a + 1) * HALF)
+
+        row_scale = kept("row_scale", [P, TOKEN_PASSES, PACK], F32)
+        m_sb = kept("m_sb", [P, COLUMN_PASSES, PACK], BF16)
+        first_bytes = [kept("xbytes0_%d" % t, [P, DI], U8) for t in range(PACK)]
+        pass_bytes = {q: kept("xbytes%d" % q, [P, PACK, DI], U8) for q in range(1, TOKEN_PASSES)}
+        g_sb = {(h, q): kept("g%d_%d" % (h, q), [P, PACK, K_PASS], BF16)
+                for h in range(COLUMN_PASSES) for q in range(TOKEN_PASSES)}
+        v_sb = [kept("v%d" % h, [P, ROW_TILES, K_PASS], BF16) for h in range(COLUMN_PASSES)]
         b_sb = kept("b_sb", [P, R // P, DO], BF16)
-        x_codes = [kept("xc%d" % q, [P, DI], U32) for q in range(NQ)]
-        x_scales = [kept("xsc%d" % q, [P, DI], U8) for q in range(NQ)]
-        g_codes = {(r, q): kept("gc%d_%d" % (r, q), [P, 2 * P], U32) for r in range(4) for q in range(NQ)}
-        g_scales = {(r, q): kept("gsc%d_%d" % (r, q), [P, 2 * P], U8) for r in range(4) for q in range(NQ)}
-        dv_codes = [kept("dc%d" % h, [P, DI], U32) for h in range(NH)]
-        dv_scales = [kept("dsc%d" % h, [P, DI], U8) for h in range(NH)]
-        b_codes = kept("bc", [P, NH * R], U32)
-        b_scales = kept("bsc", [P, NH * R], U8)
-        dv = [kept("dv%d" % h, [P, DI // CH, PACK, CH], BF16) for h in range(NH)]
-        ident_f = kept("ident_f", [P, P], F32)
-        warm = kept("warm", [P, 1], F32)
-        mask = kept("mask", [P, PACK, P // PACK], F32)
+        x_codes = [kept("x_codes%d" % q, [P, DI], U32) for q in range(TOKEN_PASSES)]
+        x_scales = [kept("x_scales%d" % q, [P, DI], U8) for q in range(TOKEN_PASSES)]
+        g_codes = {(r, q): kept("g_codes%d_%d" % (r, q), [P, 2 * P], U32)
+                   for r in range(PAIRS) for q in range(TOKEN_PASSES)}
+        g_scales = {(r, q): kept("g_scales%d_%d" % (r, q), [P, 2 * P], U8)
+                    for r in range(PAIRS) for q in range(TOKEN_PASSES)}
+        dv_codes = [kept("dv_codes%d" % h, [P, DI], U32) for h in range(COLUMN_PASSES)]
+        dv_scales = [kept("dv_scales%d" % h, [P, DI], U8) for h in range(COLUMN_PASSES)]
+        b_codes = kept("b_codes", [P, COLUMN_PASSES * R], U32)
+        b_scales = kept("b_scales", [P, COLUMN_PASSES * R], U8)
+        dv = [kept("dv%d" % h, [P, DI // QUARTER, PACK, QUARTER], BF16) for h in range(COLUMN_PASSES)]
+        identity = kept("identity", [P, P], F32)
         ones = kept("ones", [P, 2], F32)
-        masked = kept("masked", [P, PACK, P], F32)
-        rn2 = [kept("rn2_%d" % h, [P, PACK], F32) for h in range(NH)]
-        rn = [kept("rn_%d" % h, [P, PACK], F32) for h in range(NH)]
-        nalpha = [kept("na_%d" % h, [P, PACK], F32) for h in range(NH)]
-        gam = kept("gam", [P, NJ], F32)
-        part = kept("part", [P, NJ, 2], F32)
+        diagonal_mask = kept("diagonal_mask", [P, PACK, P // PACK], F32)
+        ones_squared = kept("ones_squared", [P, 2], F32)
+        diagonal = kept("diagonal", [P, PACK, P], F32)
+        inv_n2 = [kept("inv_n2_%d" % h, [P, PACK], F32) for h in range(COLUMN_PASSES)]
+        inv_n = [kept("inv_n_%d" % h, [P, PACK], F32) for h in range(COLUMN_PASSES)]
+        factor_a = [kept("factor_a%d" % h, [P, PACK], F32) for h in range(COLUMN_PASSES)]
+        factor_w = kept("factor_w", [P, TILES], F32)
+        half_sums = kept("half_sums", [P, TILES, 2], F32)
+
+        def token_rows(tensor, q):
+            return tensor[q * K_PASS:(q + 1) * K_PASS, :].rearrange("(p t) w -> p t w", t=PACK)
 
         def load_x(q):
-            nc.sync.dma_start(out=xb[q][:], in_=x_bytes[q * KP:(q + 1) * KP, :].rearrange("(p j) w -> p j w", j=PACK))
-
-        def load_x0(a):
-            nc.sync.dma_start(out=xb0[a][:], in_=x_bytes[0:KP, :].rearrange("(p j) w -> p j w", j=PACK)[:, a, :])
+            nc.sync.dma_start(out=pass_bytes[q][:], in_=token_rows(x_bytes, q))
 
         def load_g(h, q):
-            nc.sync.dma_start(out=g_raw[h, q][:],
-                              in_=g[q * KP:(q + 1) * KP, h * KP:(h + 1) * KP].rearrange("(p j) w -> p j w", j=PACK))
+            nc.sync.dma_start(out=g_sb[h, q][:], in_=token_rows(g, q)[:, :, h * K_PASS:(h + 1) * K_PASS])
 
         def load_v(h):
-            nc.sync.dma_start(out=v_sb[h][:], in_=v[:, h * KP:(h + 1) * KP].rearrange("(a p) o -> p a o", p=P))
+            nc.sync.dma_start(out=v_sb[h][:],
+                              in_=v[:, h * K_PASS:(h + 1) * K_PASS].rearrange("(n p) o -> p n o", p=P))
 
-        nc.scalar.dma_start(out=xs[:], in_=x_scale.rearrange("(q p j) o -> p q (j o)", p=P, j=PACK))
-        for j in range(PACK):
-            load_x0(j)
+        nc.scalar.dma_start(out=row_scale[:], in_=x_scale.rearrange("(q p t) o -> p q (t o)", p=P, t=PACK))
+        for t in range(PACK):
+            nc.sync.dma_start(out=first_bytes[t][:], in_=token_rows(x_bytes, 0)[:, t, :])
         load_x(1)
         load_g(0, 0)
         load_x(2)
@@ -98,370 +112,347 @@ def tile_doradirectiongradienttoloradown_kernel(tc, x_bytes, x_scale, g, v, m, b
         load_g(0, 3)
         load_v(1)
         nc.sync.dma_start(out=m_sb[:], in_=m.rearrange("(h p t) -> p h t", p=P, t=PACK))
-        for q in range(NQ):
+        for q in range(TOKEN_PASSES):
             load_g(1, q)
-        nc.sync.dma_start(out=b_sb[:], in_=b.rearrange("(c p) o -> p c o", p=P))
+        nc.sync.dma_start(out=b_sb[:], in_=b.rearrange("(n p) o -> p n o", p=P))
 
-        nc.gpsimd.memset(ones[:], 1.0)
-        nc.scalar.activation(out=warm[:], in_=ones[:, 0:1], func=ACT.Sqrt)
-        make_identity(nc, ident_f[:])
-        nc.vector.tensor_copy(out=mask[:], in_=ident_f[:].rearrange("p (n t) -> p t n", t=PACK))
+        nc.gpsimd.memset(ones_squared[:], 1.0)
+        nc.scalar.activation(out=ones[:], in_=ones_squared[:], func=ACT.Sqrt)
+        make_identity(nc, identity[:])
+        nc.vector.tensor_copy(out=diagonal_mask[:], in_=identity[:].rearrange("p (y t) -> p t y", t=PACK))
 
-        def copy(eng, out_ap, in_ap):
-            if eng == "V":
-                nc.vector.tensor_copy(out=out_ap, in_=in_ap)
-            elif eng == "G":
-                nc.gpsimd.tensor_scalar(out=out_ap, in0=in_ap, scalar1=1.0, scalar2=0.0, op0=ALU.mult, op1=ALU.add)
-            else:
-                nc.scalar.copy(out=out_ap, in_=in_ap)
+        def on_vector(out_ap, in_ap):
+            nc.vector.tensor_copy(out=out_ap, in_=in_ap)
 
-        def quantize(codes, scales, src):
-            nc.vector.quantize_mx(out=codes.bitcast(FP8X4), scales=scales, in_=src)
+        def on_scalar(out_ap, in_ap):
+            nc.scalar.copy(out=out_ap, in_=in_ap)
+
+        def on_gpsimd(out_ap, in_ap):
+            nc.gpsimd.tensor_scalar(out=out_ap, in0=in_ap, scalar1=1.0, scalar2=0.0, op0=ALU.mult, op1=ALU.add)
+
+        def quantize(codes, scales, interleaved):
+            nc.vector.quantize_mx(out=codes.bitcast(FP8X4), scales=scales, in_=interleaved)
 
         def widen(q, a):
-            xw = work.tile([P, PACK, HALF], BF16, name="xw", bufs=4, align_bytes=64)
-            for j in range(PACK):
-                src = (xb0[j][:] if q == 0 else xb[q][:, j])[:, a * HALF:(a + 1) * HALF]
-                if (q, a) == (0, 0) and j >= PACK - HEAD_V:
-                    nc.vector.tensor_scalar(out=xw[:, j, :], in0=src.bitcast(FP8), scalar1=xs[:, q, j:j + 1], scalar2=None,
-                                            op0=ALU.mult)
+            widened = rotating("widened", WIDENED_SLOTS, [P, PACK, HALF], BF16)
+            for t in range(PACK):
+                row = first_bytes[t][:] if q == 0 else pass_bytes[q][:, t]
+                values = row[:, half(a)].bitcast(FP8)
+                scale = row_scale[:, q, t:t + 1]
+                if (q, a) == (0, 0):
+                    nc.vector.tensor_scalar(out=widened[:, t, :], in0=values, scalar1=scale, scalar2=None, op0=ALU.mult)
                 else:
-                    nc.scalar.activation(out=xw[:, j, :], in_=src.bitcast(FP8), func=ACT.Copy, scale=xs[:, q, j:j + 1])
-            return xw
+                    nc.scalar.activation(out=widened[:, t, :], in_=values, func=ACT.Copy, scale=scale)
+            return widened
 
-        def interleave(eng, planes, width, name, bufs):
-            il = work.tile([P, width * PACK], BF16, name=name, bufs=bufs, align_bytes=64)
-            if eng == "G":
-                copy(eng, il[:].rearrange("p (c t) -> p c t", t=PACK), planes.rearrange("p t c -> p c t"))
-            else:
-                copy(eng, il[:].rearrange("p (c i t) -> p c t i", i=4, t=PACK),
-                     planes.rearrange("p t (c i) -> p c t i", i=4))
-            return il
+        def interleave(copy, rows, interleaved):
+            copy(interleaved[:].rearrange("p (y i t) -> p y t i", i=RUN, t=PACK),
+                 rows.rearrange("p t (y i) -> p y t i", i=RUN))
 
-        g_il = {}
+        def interleave_x(widened):
+            interleaved = rotating("wide", WIDE_SLOTS, [P, HALF * PACK], BF16)
+            interleave(on_vector, widened[:], interleaved)
+            return interleaved
 
-        def interleave_g(eng, r, q, gate=False):
+        def quantize_x(q, a, interleaved):
+            quantize(x_codes[q][:, half(a)], x_scales[q][:, half(a)], interleaved[:])
+
+        def piece():
+            return rotating("piece", PIECE_SLOTS, [P, QUARTER * PACK], BF16)
+
+        def turn_piece():
+            return rotating("turn_piece", 1, [P, QUARTER * PACK], BF16)
+
+        g_pieces = {}
+
+        def interleave_g(copy, r, q, interleaved):
             h, u = divmod(r, 2)
-            if eng == "G":
-                il = work.tile([P, 2 * P * PACK], BF16, name="gate", bufs=1, align_bytes=64)
-                copy(eng, il[:].rearrange("p (t c j) -> p t c j", t=2, j=PACK),
-                     g_raw[h, q][:].rearrange("p j (c u t) -> p u t c j", u=2, t=2)[:, u])
-            else:
-                il = work.tile([P, 2 * P * PACK], BF16, name="gate" if gate else "piece", bufs=1 if gate else 8, align_bytes=64)
-                copy(eng, il[:].rearrange("p (t c e j) -> p c j e t", t=2, e=2, j=PACK),
-                     g_raw[h, q][:].rearrange("p j (c e u t) -> p u c j e t", e=2, u=2, t=2)[:, u])
-            g_il[r, q] = il
+            copy(interleaved[:].rearrange("p (e y z t) -> p y t z e", e=2, z=2, t=PACK),
+                 g_sb[h, q][:].rearrange("p t (y z u e) -> p u y t z e", z=2, u=2, e=2)[:, u])
+            g_pieces[r, q] = interleaved
+
+        def interleave_g_on_gpsimd(r, q):
+            h, u = divmod(r, 2)
+            g_pieces[r, q] = turn_piece()
+            on_gpsimd(g_pieces[r, q][:].rearrange("p (e s t) -> p e s t", e=2, t=PACK),
+                      g_sb[h, q][:].rearrange("p t (s u e) -> p u e s t", u=2, e=2)[:, u])
 
         def quantize_g(r, q):
-            quantize(g_codes[r, q][:], g_scales[r, q][:], g_il[r, q][:])
+            quantize(g_codes[r, q][:], g_scales[r, q][:], g_pieces[r, q][:])
 
-        def quantize_x(q, a, il):
-            cols = slice(a * HALF, (a + 1) * HALF)
-            quantize(x_codes[q][:, cols], x_scales[q][:, cols], il[:])
+        def quantize_pair(r):
+            for q in range(TOKEN_PASSES):
+                quantize_g(r, q)
 
-        acc = {}
+        gw = {}
 
-        def product(j, a, passes):
-            r, t = divmod(j, 2)
-            if (j, a) not in acc:
-                acc[j, a] = bank(2 * (j % 2) + a, "acc", [P, HALF], F32)
-            oc = slice(t * P, (t + 1) * P)
-            ic = slice(a * HALF, (a + 1) * HALF)
-            for q in passes:
-                nc.tensor.matmul_mx(out=acc[j, a][:], lhsT=g_codes[r, q][:, oc].bitcast(FP8X4), lhsT_scale=g_scales[r, q][:, oc],
-                                    rhs=x_codes[q][:, ic].bitcast(FP8X4), rhs_scale=x_scales[q][:, ic],
-                                    start=(q == 0), stop=(q == NQ - 1))
+        def product(j, a, q):
+            r, e = divmod(j, 2)
+            if q == 0:
+                gw[j, a] = bank(2 * e + a, "gw", [P, HALF], F32)
+            columns = slice(e * P, (e + 1) * P)
+            nc.tensor.matmul_mx(out=gw[j, a][:],
+                                lhsT=g_codes[r, q][:, columns].bitcast(FP8X4), lhsT_scale=g_scales[r, q][:, columns],
+                                rhs=x_codes[q][:, half(a)].bitcast(FP8X4), rhs_scale=x_scales[q][:, half(a)],
+                                start=(q == 0), stop=(q == LAST))
+
+        def first_pair_pass(q):
+            for a in range(2):
+                product(0, a, q)
+                product(1, a, q)
 
         def product_tile(j):
-            product(j, 0, range(NQ))
-            product(j, 1, range(NQ))
+            for a in range(2):
+                for q in range(TOKEN_PASSES):
+                    product(j, a, q)
 
         gram = {}
-
-        def gram_products(h):
-            gram[h] = bank(4 + h, "gram", [P, PACK, P], F32)
-            for t in range(PACK):
-                for c in range(DI // P):
-                    cols = v_sb[h][:, c, t * P:(t + 1) * P]
-                    nc.tensor.matmul(out=gram[h][:, t, :], lhsT=cols, rhs=cols, start=(c == 0), stop=(c == DI // P - 1))
-
-        def mask_gram(h):
-            nc.vector.tensor_tensor(out=masked[:].rearrange("p t (c n) -> p t c n", c=PACK),
-                                    in0=gram[h][:].rearrange("p c (n t) -> p t c n", t=PACK),
-                                    in1=mask[:].unsqueeze(2).broadcast_to([P, PACK, PACK, P // PACK]), op=ALU.mult)
-
         n2 = {}
 
-        def column_sums(h):
+        def gram_blocks(h):
+            gram[h] = bank(4 + h, "gram", [P, PACK, P], F32)
+            for block in range(PACK):
+                for n in range(ROW_TILES):
+                    columns = v_sb[h][:, n, block * P:(block + 1) * P]
+                    nc.tensor.matmul(out=gram[h][:, block, :], lhsT=columns, rhs=columns,
+                                     start=(n == 0), stop=(n == ROW_TILES - 1))
+
+        def take_diagonal(h):
+            nc.vector.tensor_tensor(out=diagonal[:].rearrange("p t (block y) -> p t block y", block=PACK),
+                                    in0=gram[h][:].rearrange("p block (y t) -> p t block y", t=PACK),
+                                    in1=diagonal_mask[:].unsqueeze(2).broadcast_to([P, PACK, PACK, P // PACK]),
+                                    op=ALU.mult)
             n2[h] = bank(4 + h, "n2", [P, PACK, 2], F32)
             for t in range(PACK):
-                nc.tensor.matmul(out=n2[h][:, t, :], lhsT=masked[:, t, :], rhs=ones[:], start=True, stop=True)
+                nc.tensor.matmul(out=n2[h][:, t, :], lhsT=diagonal[:, t, :], rhs=ones[:], start=True, stop=True)
 
-        def recip(h):
-            nc.vector.reciprocal(out=rn2[h][:], in_=n2[h][:, :, 0])
+        def invert_n2(h):
+            nc.vector.reciprocal(out=inv_n2[h][:], in_=n2[h][:, :, 0])
 
         def root(h):
-            nc.scalar.activation(out=rn[h][:], in_=rn2[h][:], func=ACT.Sqrt)
+            nc.scalar.activation(out=inv_n[h][:], in_=inv_n2[h][:], func=ACT.Sqrt)
 
-        def alpha(h):
-            nc.vector.scalar_tensor_tensor(out=nalpha[h][:], in0=rn[h][:], scalar=-1.0, in1=m_sb[:, h, :],
+        def make_factor_a(h):
+            nc.vector.scalar_tensor_tensor(out=factor_a[h][:], in0=inv_n[h][:], scalar=-1.0, in1=m_sb[:, h, :],
                                            op0=ALU.mult, op1=ALU.mult)
 
-        vt = {}
+        v_words = {}
 
         def turn_v(r):
             h, u = divmod(r, 2)
-            words = v_sb[h][:].rearrange("p c o -> p (c o)").bitcast(F32)
+            words = v_sb[h][:].rearrange("p n o -> p (n o)").bitcast(F32)
             for a in range(2):
-                vt[r, a] = bank(4 + 2 * ((r + 1) % 2) + a, "vt", [P, HALF], F32)
-                for c in range(HALF // P):
-                    w0 = (a * (HALF // P) + c) * (KP // 2)
-                    nc.tensor.transpose(vt[r, a][:, c * P:(c + 1) * P], words[:, w0 + u:w0 + KP // 2:2], ident_f[:])
+                v_words[r, a] = bank(4 + 2 * ((r + 1) % 2) + a, "v_words", [P, HALF], F32)
+                for n in range(HALF // P):
+                    first = (a * (HALF // P) + n) * (K_PASS // 2)
+                    nc.tensor.transpose(v_words[r, a][:, n * P:(n + 1) * P],
+                                        words[:, first + u:first + K_PASS // 2:2], identity[:])
 
         def v_t(j, a):
-            return vt[j // 2, a][:].bitcast(BF16)[:, j % 2:2 * HALF:2]
+            return v_words[j // 2, a][:].bitcast(BF16)[:, j % 2:2 * HALF:2]
 
-        gs = {}
+        scaled = {}
 
-        def scale_out(j, a):
+        def scale_tile(j):
             h, t = divmod(j, PACK)
-            if a == 0:
-                gs[j] = work.tile([P, DI], F32, name="gs", bufs=5, align_bytes=64)
-            nc.scalar.activation(out=gs[j][:, a * HALF:(a + 1) * HALF], in_=acc[j, a][:], func=ACT.Copy,
-                                 scale=nalpha[h][:, t:t + 1])
+            scaled[j] = rotating("scaled", SCALED_SLOTS, [P, DI], F32)
+            for a in range(2):
+                nc.scalar.activation(out=scaled[j][:, half(a)], in_=gw[j, a][:], func=ACT.Copy,
+                                     scale=factor_a[h][:, t:t + 1])
 
         def project(j, a):
             h, t = divmod(j, PACK)
-            junk = work.tile([P, HALF], F32, name="junk", bufs=2, align_bytes=64)
-            nc.vector.scalar_tensor_tensor(out=junk[:], in0=v_t(j, a), scalar=rn2[h][:, t:t + 1],
-                                           in1=gs[j][:, a * HALF:(a + 1) * HALF],
-                                           op0=ALU.mult, op1=ALU.mult, accum_out=part[:, j, a:a + 1])
+            summands = rotating("summands", 2, [P, HALF], F32)
+            nc.vector.scalar_tensor_tensor(out=summands[:], in0=v_t(j, a), scalar=inv_n2[h][:, t:t + 1],
+                                           in1=scaled[j][:, half(a)], op0=ALU.mult, op1=ALU.mult,
+                                           accum_out=half_sums[:, j, a:a + 1])
 
-        def join(r):
-            j = slice(2 * r, 2 * r + 2)
-            nc.vector.tensor_tensor(out=gam[:, j], in0=part[:, j, 0], in1=part[:, j, 1], op=ALU.add)
+        def join(j):
+            nc.vector.tensor_scalar(out=factor_w[:, j:j + 1], in0=half_sums[:, j, 0:1], scalar1=half_sums[:, j, 1:2],
+                                    scalar2=None, op0=ALU.add)
 
-        def combine(j, c0, c1):
+        def chunks(ap):
+            return ap.rearrange("p (c i) -> p c i", i=QUARTER)
+
+        def combine(j, c, count):
             h, t = divmod(j, PACK)
-            a = c0 // 2
-            nc.vector.scalar_tensor_tensor(out=dv[h][:, c0:c1, t, :],
-                                           in0=v_t(j, a)[:, (c0 - 2 * a) * CH:(c1 - 2 * a) * CH].rearrange("p (c i) -> p c i", i=CH),
-                                           scalar=gam[:, j:j + 1],
-                                           in1=gs[j][:, c0 * CH:c1 * CH].rearrange("p (c i) -> p c i", i=CH),
+            a, within = divmod(c, 2)
+            nc.vector.scalar_tensor_tensor(out=dv[h][:, c:c + count, t, :],
+                                           in0=chunks(v_t(j, a)[:, within * QUARTER:(within + count) * QUARTER]),
+                                           scalar=factor_w[:, j:j + 1],
+                                           in1=chunks(scaled[j][:, c * QUARTER:(c + count) * QUARTER]),
                                            op0=ALU.mult, op1=ALU.subtract)
 
-        def projections(r):
-            j = 2 * r
-            project(j, 0)
-            project(j + 1, 0)
-            project(j, 1)
-            project(j + 1, 1)
-            join(r)
+        def combine_half(j, a):
+            combine(j, 2 * a, 2)
 
-        def combinations(r):
-            for j in (2 * r, 2 * r + 1):
-                combine(j, 0, 2)
-                combine(j, 2, 4)
+        def combine_half_off_vector(j, a):
+            h, t = divmod(j, PACK)
+            along_v = rotating("along_v", 1, [P, HALF], F32)
+            nc.scalar.activation(out=along_v[:], in_=v_t(j, a), func=ACT.Copy, scale=factor_w[:, j:j + 1])
+            nc.gpsimd.tensor_tensor(out=dv[h][:, 2 * a:2 * a + 2, t, :], in0=chunks(along_v[:]),
+                                    in1=chunks(scaled[j][:, half(a)]), op=ALU.subtract)
 
-        def pair(r, jobs, last=False):
+        def project_pair(r):
             j = 2 * r
             project(j, 0)
             project(j, 1)
             project(j + 1, 0)
-            join1(j)
+            join(j)
             project(j + 1, 1)
-            if last:
-                jobs()
-                join1(j + 1)
-            else:
-                combine(j, 0, 2)
-                join1(j + 1)
-                if LATE[r]:
-                    combine(j, 2, 4)
-                    jobs()
-                else:
-                    jobs()
-                    combine(j, 2, 4)
-                combine(j + 1, 0, 2)
-                combine(j + 1, 2, 4)
 
-        def join1(j):
-            nc.vector.tensor_tensor(out=gam[:, j:j + 1], in0=part[:, j, 0:1], in1=part[:, j, 1:2], op=ALU.add)
+        dv_pieces = {}
 
-        def scale_tile(j):
-            scale_out(j, 0)
-            scale_out(j, 1)
+        def interleave_dv(copy, h, c):
+            dv_pieces[h, c] = piece()
+            interleave(copy, dv[h][:, c], dv_pieces[h, c])
 
-        def products(r):
-            for a in range(2):
-                product(2 * r, a, range(NQ))
-                product(2 * r + 1, a, range(NQ))
+        def interleave_dv_on_gpsimd(h, c):
+            dv_pieces[h, c] = turn_piece()
+            on_gpsimd(dv_pieces[h, c][:].rearrange("p (i t) -> p i t", t=PACK), dv[h][:, c].rearrange("p t i -> p i t"))
 
-        def scale_half(r, a):
-            scale_out(2 * r, a)
-            scale_out(2 * r + 1, a)
-
-        def quantize_dv(h, i0, width, il):
-            quantize(dv_codes[h][:, i0:i0 + width], dv_scales[h][:, i0:i0 + width], il[:])
-
-        dv_il = {}
-
-        def interleave_dv(eng, h, c):
-            dv_il[h, c] = interleave(eng, dv[h][:, c], CH, *(("gate", 1) if eng == "G" else ("piece", 8)))
-
-        def quantize_dv_piece(h, c):
-            quantize_dv(h, c * CH, CH, dv_il[h, c])
+        def quantize_dv(h, c):
+            rows = slice(c * QUARTER, (c + 1) * QUARTER)
+            quantize(dv_codes[h][:, rows], dv_scales[h][:, rows], dv_pieces[h, c][:])
 
         def turn_b():
-            b_words = b_sb[:].rearrange("p c o -> p (c o)").bitcast(F32)
-            b_il = work.tile([P, NH * R * PACK], BF16, name="il", bufs=3, align_bytes=64)
-            b_il_words = b_il[:].bitcast(F32)
-            for h in range(NH):
-                bt = bank(h, "bt", [P, R // P, 2, P], F32)
-                for c in range(R // P):
+            words = b_sb[:].rearrange("p n o -> p (n o)").bitcast(F32)
+            interleaved = rotating("wide", WIDE_SLOTS, [P, COLUMN_PASSES * R * PACK], BF16)
+            interleaved_words = interleaved[:].bitcast(F32)
+            for h in range(COLUMN_PASSES):
+                b_words = bank(h, "b_words", [P, R // P, 2, P], F32)
+                for n in range(R // P):
                     for u in range(2):
-                        w0 = c * (DO // 2) + h * (KP // 2)
-                        nc.tensor.transpose(bt[:, c, u, :], b_words[:, w0 + u:w0 + KP // 2:2], ident_f[:])
-                nc.scalar.copy(out=b_il_words[:, h * 2 * R:(h + 1) * 2 * R].rearrange("p (c r u) -> p c r u", c=R // P, u=2),
-                               in_=bt[:].rearrange("p c u r -> p c r u"))
-            return b_il
+                        first = n * (DO // 2) + h * (K_PASS // 2)
+                        nc.tensor.transpose(b_words[:, n, u, :], words[:, first + u:first + K_PASS // 2:2], identity[:])
+                on_scalar(interleaved_words[:, h * 2 * R:(h + 1) * 2 * R].rearrange("p (n row u) -> p n row u", n=R // P, u=2),
+                          b_words[:].rearrange("p n u row -> p n row u"))
+            return interleaved
 
-        for q in range(NQ):
-            xw = [widen(q, 0), widen(q, 1)]
-            xi0 = interleave("V", xw[0][:], HALF, "il", 3)
-            if q == 0:
-                xi1 = interleave("V", xw[1][:], HALF, "il", 3)
-                quantize_x(q, 0, xi0)
-                interleave_g("V", 0, q)
-                quantize_x(q, 1, xi1)
-                quantize_g(0, q)
-                for a in range(2):
-                    product(0, a, [q])
-                    product(1, a, [q])
-                gram_products(0)
-                continue
-            interleave_g("S" if q == 3 else "V", 0, q)
-            if q == 3:
+        out_sums = {}
+
+        def second_product(n, h):
+            if h == 0:
+                out_sums[n] = bank(OUT_BANKS[n], "out_sums", [P, R], F32)
+            rows = slice(n * P, (n + 1) * P)
+            columns = slice(h * R, (h + 1) * R)
+            nc.tensor.matmul_mx(out=out_sums[n][:],
+                                lhsT=dv_codes[h][:, rows].bitcast(FP8X4), lhsT_scale=dv_scales[h][:, rows],
+                                rhs=b_codes[:, columns].bitcast(FP8X4), rhs_scale=b_scales[:, columns],
+                                start=(h == 0), stop=(h == COLUMN_PASSES - 1))
+
+        def finish(c, copies):
+            for n, copy in zip((2 * c, 2 * c + 1), copies):
+                second_product(n, 1)
+                result = rotating("result", ROW_TILES, [P, R], F32)
+                copy(result[:], out_sums[n][:])
+                nc.sync.dma_start(out=out[n * P:(n + 1) * P, :], in_=result[:])
+
+        widened = [widen(0, 0), widen(0, 1)]
+        x_halves = [interleave_x(widened[0]), interleave_x(widened[1])]
+        quantize_x(0, 0, x_halves[0])
+        interleave_g(on_vector, 0, 0, piece())
+        quantize_x(0, 1, x_halves[1])
+        quantize_g(0, 0)
+        first_pair_pass(0)
+        gram_blocks(0)
+        for q in range(1, TOKEN_PASSES):
+            widened = [widen(q, 0), widen(q, 1)]
+            first_half = interleave_x(widened[0])
+            if q < LAST:
+                interleave_g(on_vector, 0, q, piece())
+            else:
+                interleave_g(on_scalar, 0, q, piece())
                 root(0)
-            quantize_x(q, 0, xi0)
-            if q == 2:
-                mask_gram(0)
-                column_sums(0)
-            xi1 = interleave("V", xw[1][:], HALF, "il", 3)
+            quantize_x(q, 0, first_half)
+            if q == LAST - 1:
+                take_diagonal(0)
+            second_half = interleave_x(widened[1])
             quantize_g(0, q)
-            if q == 3:
-                alpha(0)
-            quantize_x(q, 1, xi1)
-            if q == 2:
-                recip(0)
-            for a in range(2):
-                product(0, a, [q])
-                product(1, a, [q])
-            if q == 0:
-                gram_products(0)
+            if q == LAST:
+                make_factor_a(0)
+            quantize_x(q, 1, second_half)
+            if q == LAST - 1:
+                invert_n2(0)
+            first_pair_pass(q)
             if q == 1:
                 turn_v(0)
-            if q == 2:
-                gram_products(1)
-        for q in range(3):
-            interleave_g("S", 1, q)
-        mask_gram(1)
-        column_sums(1)
-        interleave_g("S", 1, 3, True)
-        for q in range(NQ):
-            quantize_g(1, q)
+            if q == LAST - 1:
+                gram_blocks(1)
+
+        for q in range(LAST):
+            interleave_g(on_scalar, 1, q, piece())
+        take_diagonal(1)
+        interleave_g(on_vector, 1, LAST, turn_piece())
+        quantize_pair(1)
         scale_tile(0)
         scale_tile(1)
-        recip(1)
+        invert_n2(1)
         root(1)
         product_tile(2)
         turn_v(1)
         product_tile(3)
-        interleave_g("V", 2, 3)
-        for q in range(3):
-            interleave_g("S", 2, q)
+        for r in range(2):
+            j = 2 * r
+            interleave_g_on_gpsimd(r + 2, LAST)
+            for q in range(LAST):
+                interleave_g(on_scalar, r + 2, q, piece())
+            if r == 0:
+                scale_tile(2)
+                scale_tile(3)
+            project_pair(r)
+            combine_half(j, 0)
+            join(j + 1)
+            combine_half(j, 1)
+            if r == 0:
+                make_factor_a(1)
+            quantize_pair(r + 2)
+            combine_half(j + 1, 0)
+            combine_half(j + 1, 1)
+            if r == 1:
+                scale_tile(4)
+                scale_tile(5)
+            product_tile(j + 4)
+            turn_v(r + 2)
+            product_tile(j + 5)
 
-        def jobs0():
-            alpha(1)
-            for q in (0, 1, 2, 3):
-                quantize_g(2, q)
-
-        scale_tile(2)
-        scale_tile(3)
-        pair(0, jobs0)
-        product_tile(4)
-        turn_v(2)
-        product_tile(5)
-        interleave_g("V", 3, 3)
-        for q in range(3):
-            interleave_g("S", 3, q)
-
-        def jobs1():
-            for q in (0, 1, 2, 3):
-                quantize_g(3, q)
-
-        pair(1, jobs1)
-        scale_tile(4)
-        scale_tile(5)
-        product_tile(6)
-        turn_v(3)
-        product_tile(7)
-        interleave_dv("S", 0, 0)
-        interleave_dv("S", 0, 1)
+        interleave_dv_on_gpsimd(0, 0)
+        interleave_dv(on_scalar, 0, 1)
         scale_tile(6)
-        interleave_dv("S", 0, 2)
-
-        def jobs2():
-            quantize_dv_piece(0, 1)
-            quantize_dv_piece(0, 0)
-
-        pair(2, jobs2)
+        interleave_dv(on_scalar, 0, 2)
+        project_pair(2)
+        combine_half(4, 0)
+        join(5)
+        quantize_dv(0, 1)
+        quantize_dv(0, 0)
+        combine_half(4, 1)
+        combine_half(5, 0)
         scale_tile(7)
-        interleave_dv("S", 0, 3)
-        b_il = turn_b()
+        combine_half_off_vector(5, 1)
+        interleave_dv(on_scalar, 0, 3)
+        b_interleaved = turn_b()
 
-        def jobs3():
-            quantize_dv_piece(0, 2)
-            quantize_dv_piece(0, 3)
-            quantize(b_codes[:], b_scales[:], b_il[:])
-
-        pair(3, jobs3, True)
-        for c in range(DI // CH):
-            combine(6, c, c + 1)
-            combine(7, c, c + 1)
-
-        out_banks = [6, 7, 0, 1, 2, 3, 4, 5]
-        o_acc = {}
-
-        def second(n, h):
-            i0 = n * P
-            if h == 0:
-                o_acc[n] = bank(out_banks[n], "oacc", [P, R], F32)
-            nc.tensor.matmul_mx(out=o_acc[n][:], lhsT=dv_codes[h][:, i0:i0 + P].bitcast(FP8X4),
-                                lhsT_scale=dv_scales[h][:, i0:i0 + P],
-                                rhs=b_codes[:, h * R:(h + 1) * R].bitcast(FP8X4),
-                                rhs_scale=b_scales[:, h * R:(h + 1) * R],
-                                start=(h == 0), stop=(h == NH - 1))
-
-        def finish(c, engines):
-            for k in range(2):
-                n = 2 * c + k
-                second(n, 1)
-                res = work.tile([P, R], F32, name="res", bufs=8, align_bytes=64)
-                copy(engines[k], res[:], o_acc[n][:])
-                nc.sync.dma_start(out=out[n * P:(n + 1) * P, :], in_=res[:])
-
-        for n in range(DI // P):
-            second(n, 0)
-        interleave_dv("S", 1, 0)
-        interleave_dv("S", 1, 1)
-        interleave_dv("S", 1, 2)
-        quantize_dv_piece(1, 0)
-        interleave_dv("V", 1, 3)
-        quantize_dv_piece(1, 1)
-        finish(0, "VV")
-        quantize_dv_piece(1, 3)
-        quantize_dv_piece(1, 2)
-        finish(1, "SS")
-        finish(3, "SV")
-        finish(2, "SV")
+        project_pair(3)
+        quantize_dv(0, 2)
+        join(7)
+        for c in range(DI // QUARTER):
+            combine(6, c, 1)
+            combine(7, c, 1)
+            if c < 3:
+                interleave_dv(on_scalar, 1, c)
+            if c == 0:
+                quantize_dv(0, 3)
+                quantize(b_codes[:], b_scales[:], b_interleaved[:])
+                for n in range(EARLY_OUT_TILES):
+                    second_product(n, 0)
+            if c == 2:
+                quantize_dv(1, 0)
+        finish(0, (on_scalar, on_scalar))
+        for n in range(EARLY_OUT_TILES, ROW_TILES):
+            second_product(n, 0)
+        quantize_dv(1, 1)
+        interleave_dv(on_vector, 1, 3)
+        quantize_dv(1, 2)
+        quantize_dv(1, 3)
+        for c in range(1, DI // QUARTER):
+            finish(c, (on_scalar, on_vector))

from contextlib import ExitStack

import concourse.mybir as mybir
from concourse.masks import make_identity

T, DI, DO, R = 2048, 1024, 1024, 256
FLOPS = 2 * T * DI * DO + 2 * DI * DO * R

F32 = mybir.dt.float32
BF16 = mybir.dt.bfloat16
U32 = mybir.dt.uint32
U8 = mybir.dt.uint8
FP8 = mybir.dt.float8_e4m3fn
FP8X4 = mybir.dt.float8_e4m3fn_x4
ACT = mybir.ActivationFunctionType
ALU = mybir.AluOpType

P = 128
PACK = 4
K_PASS = P * PACK
TOKEN_PASSES = T // K_PASS
COLUMN_PASSES = DO // K_PASS
TILES = COLUMN_PASSES * PACK
PAIRS = TILES // 2
HALF = DI // 2
QUARTER = DI // 4
ROW_TILES = DI // P
RUN = 4
LAST = TOKEN_PASSES - 1

WIDENED_SLOTS = 4
WIDE_SLOTS = 3
PIECE_SLOTS = 8
SCALED_SLOTS = 5
OUT_BANKS = (6, 7, 0, 1, 2, 3, 4, 5)
EARLY_OUT_TILES = 6


def tile_doradirectiongradienttoloradown_kernel(tc, x_bytes, x_scale, g, v, m, b, out):
    nc = tc.nc
    with ExitStack() as ctx:
        keep = ctx.enter_context(tc.tile_pool(name="keep", bufs=1))
        work = ctx.enter_context(tc.tile_pool(name="work", bufs=1))
        psum = ctx.enter_context(tc.psum_pool(name="psum", bufs=1))
        ctx.enter_context(tc.manual_schedule())

        def kept(name, shape, dtype):
            return keep.tile(shape, dtype, name=name, align_bytes=64)

        def rotating(name, slots, shape, dtype):
            return work.tile(shape, dtype, name=name, bufs=slots, align_bytes=64)

        def bank(number, name, shape, dtype):
            return psum.tile(shape, dtype, name=name, tag="bank%d" % number)

        def half(a):
            return slice(a * HALF, (a + 1) * HALF)

        row_scale = kept("row_scale", [P, TOKEN_PASSES, PACK], F32)
        m_sb = kept("m_sb", [P, COLUMN_PASSES, PACK], BF16)
        first_bytes = [kept("xbytes0_%d" % t, [P, DI], U8) for t in range(PACK)]
        pass_bytes = {q: kept("xbytes%d" % q, [P, PACK, DI], U8) for q in range(1, TOKEN_PASSES)}
        g_sb = {(h, q): kept("g%d_%d" % (h, q), [P, PACK, K_PASS], BF16)
                for h in range(COLUMN_PASSES) for q in range(TOKEN_PASSES)}
        v_sb = [kept("v%d" % h, [P, ROW_TILES, K_PASS], BF16) for h in range(COLUMN_PASSES)]
        b_sb = kept("b_sb", [P, R // P, DO], BF16)
        x_codes = [kept("x_codes%d" % q, [P, DI], U32) for q in range(TOKEN_PASSES)]
        x_scales = [kept("x_scales%d" % q, [P, DI], U8) for q in range(TOKEN_PASSES)]
        g_codes = {(r, q): kept("g_codes%d_%d" % (r, q), [P, 2 * P], U32)
                   for r in range(PAIRS) for q in range(TOKEN_PASSES)}
        g_scales = {(r, q): kept("g_scales%d_%d" % (r, q), [P, 2 * P], U8)
                    for r in range(PAIRS) for q in range(TOKEN_PASSES)}
        dv_codes = [kept("dv_codes%d" % h, [P, DI], U32) for h in range(COLUMN_PASSES)]
        dv_scales = [kept("dv_scales%d" % h, [P, DI], U8) for h in range(COLUMN_PASSES)]
        b_codes = kept("b_codes", [P, COLUMN_PASSES * R], U32)
        b_scales = kept("b_scales", [P, COLUMN_PASSES * R], U8)
        dv = [kept("dv%d" % h, [P, DI // QUARTER, PACK, QUARTER], BF16) for h in range(COLUMN_PASSES)]
        identity = kept("identity", [P, P], F32)
        ones = kept("ones", [P, 2], F32)
        diagonal_mask = kept("diagonal_mask", [P, PACK, P // PACK], F32)
        ones_squared = kept("ones_squared", [P, 2], F32)
        diagonal = kept("diagonal", [P, PACK, P], F32)
        inv_n2 = [kept("inv_n2_%d" % h, [P, PACK], F32) for h in range(COLUMN_PASSES)]
        inv_n = [kept("inv_n_%d" % h, [P, PACK], F32) for h in range(COLUMN_PASSES)]
        factor_a = [kept("factor_a%d" % h, [P, PACK], F32) for h in range(COLUMN_PASSES)]
        factor_w = kept("factor_w", [P, TILES], F32)
        half_sums = kept("half_sums", [P, TILES, 2], F32)

        def token_rows(tensor, q):
            return tensor[q * K_PASS:(q + 1) * K_PASS, :].rearrange("(p t) w -> p t w", t=PACK)

        def load_x(q):
            nc.sync.dma_start(out=pass_bytes[q][:], in_=token_rows(x_bytes, q))

        def load_g(h, q):
            nc.sync.dma_start(out=g_sb[h, q][:], in_=token_rows(g, q)[:, :, h * K_PASS:(h + 1) * K_PASS])

        def load_v(h):
            nc.sync.dma_start(out=v_sb[h][:],
                              in_=v[:, h * K_PASS:(h + 1) * K_PASS].rearrange("(n p) o -> p n o", p=P))

        nc.scalar.dma_start(out=row_scale[:], in_=x_scale.rearrange("(q p t) o -> p q (t o)", p=P, t=PACK))
        for t in range(PACK):
            nc.sync.dma_start(out=first_bytes[t][:], in_=token_rows(x_bytes, 0)[:, t, :])
        load_x(1)
        load_g(0, 0)
        load_x(2)
        load_g(0, 1)
        load_v(0)
        load_x(3)
        load_g(0, 2)
        load_g(0, 3)
        load_v(1)
        nc.sync.dma_start(out=m_sb[:], in_=m.rearrange("(h p t) -> p h t", p=P, t=PACK))
        for q in range(TOKEN_PASSES):
            load_g(1, q)
        nc.sync.dma_start(out=b_sb[:], in_=b.rearrange("(n p) o -> p n o", p=P))

        nc.gpsimd.memset(ones_squared[:], 1.0)
        nc.scalar.activation(out=ones[:], in_=ones_squared[:], func=ACT.Sqrt)
        make_identity(nc, identity[:])
        nc.vector.tensor_copy(out=diagonal_mask[:], in_=identity[:].rearrange("p (y t) -> p t y", t=PACK))

        def on_vector(out_ap, in_ap):
            nc.vector.tensor_copy(out=out_ap, in_=in_ap)

        def on_scalar(out_ap, in_ap):
            nc.scalar.copy(out=out_ap, in_=in_ap)

        def on_gpsimd(out_ap, in_ap):
            nc.gpsimd.tensor_scalar(out=out_ap, in0=in_ap, scalar1=1.0, scalar2=0.0, op0=ALU.mult, op1=ALU.add)

        def quantize(codes, scales, interleaved):
            nc.vector.quantize_mx(out=codes.bitcast(FP8X4), scales=scales, in_=interleaved)

        def widen(q, a):
            widened = rotating("widened", WIDENED_SLOTS, [P, PACK, HALF], BF16)
            for t in range(PACK):
                row = first_bytes[t][:] if q == 0 else pass_bytes[q][:, t]
                values = row[:, half(a)].bitcast(FP8)
                scale = row_scale[:, q, t:t + 1]
                if (q, a) == (0, 0):
                    nc.vector.tensor_scalar(out=widened[:, t, :], in0=values, scalar1=scale, scalar2=None, op0=ALU.mult)
                else:
                    nc.scalar.activation(out=widened[:, t, :], in_=values, func=ACT.Copy, scale=scale)
            return widened

        def interleave(copy, rows, interleaved):
            copy(interleaved[:].rearrange("p (y i t) -> p y t i", i=RUN, t=PACK),
                 rows.rearrange("p t (y i) -> p y t i", i=RUN))

        def interleave_x(widened):
            interleaved = rotating("wide", WIDE_SLOTS, [P, HALF * PACK], BF16)
            interleave(on_vector, widened[:], interleaved)
            return interleaved

        def quantize_x(q, a, interleaved):
            quantize(x_codes[q][:, half(a)], x_scales[q][:, half(a)], interleaved[:])

        def piece():
            return rotating("piece", PIECE_SLOTS, [P, QUARTER * PACK], BF16)

        def turn_piece():
            return rotating("turn_piece", 1, [P, QUARTER * PACK], BF16)

        g_pieces = {}

        def interleave_g(copy, r, q, interleaved):
            h, u = divmod(r, 2)
            copy(interleaved[:].rearrange("p (e y z t) -> p y t z e", e=2, z=2, t=PACK),
                 g_sb[h, q][:].rearrange("p t (y z u e) -> p u y t z e", z=2, u=2, e=2)[:, u])
            g_pieces[r, q] = interleaved

        def interleave_g_on_gpsimd(r, q):
            h, u = divmod(r, 2)
            g_pieces[r, q] = turn_piece()
            on_gpsimd(g_pieces[r, q][:].rearrange("p (e s t) -> p e s t", e=2, t=PACK),
                      g_sb[h, q][:].rearrange("p t (s u e) -> p u e s t", u=2, e=2)[:, u])

        def quantize_g(r, q):
            quantize(g_codes[r, q][:], g_scales[r, q][:], g_pieces[r, q][:])

        def quantize_pair(r):
            for q in range(TOKEN_PASSES):
                quantize_g(r, q)

        gw = {}

        def product(j, a, q):
            r, e = divmod(j, 2)
            if q == 0:
                gw[j, a] = bank(2 * e + a, "gw", [P, HALF], F32)
            columns = slice(e * P, (e + 1) * P)
            nc.tensor.matmul_mx(out=gw[j, a][:],
                                lhsT=g_codes[r, q][:, columns].bitcast(FP8X4), lhsT_scale=g_scales[r, q][:, columns],
                                rhs=x_codes[q][:, half(a)].bitcast(FP8X4), rhs_scale=x_scales[q][:, half(a)],
                                start=(q == 0), stop=(q == LAST))

        def first_pair_pass(q):
            for a in range(2):
                product(0, a, q)
                product(1, a, q)

        def product_tile(j):
            for a in range(2):
                for q in range(TOKEN_PASSES):
                    product(j, a, q)

        gram = {}
        n2 = {}

        def gram_blocks(h):
            gram[h] = bank(4 + h, "gram", [P, PACK, P], F32)
            for block in range(PACK):
                for n in range(ROW_TILES):
                    columns = v_sb[h][:, n, block * P:(block + 1) * P]
                    nc.tensor.matmul(out=gram[h][:, block, :], lhsT=columns, rhs=columns,
                                     start=(n == 0), stop=(n == ROW_TILES - 1))

        def take_diagonal(h):
            nc.vector.tensor_tensor(out=diagonal[:].rearrange("p t (block y) -> p t block y", block=PACK),
                                    in0=gram[h][:].rearrange("p block (y t) -> p t block y", t=PACK),
                                    in1=diagonal_mask[:].unsqueeze(2).broadcast_to([P, PACK, PACK, P // PACK]),
                                    op=ALU.mult)
            n2[h] = bank(4 + h, "n2", [P, PACK, 2], F32)
            for t in range(PACK):
                nc.tensor.matmul(out=n2[h][:, t, :], lhsT=diagonal[:, t, :], rhs=ones[:], start=True, stop=True)

        def invert_n2(h):
            nc.vector.reciprocal(out=inv_n2[h][:], in_=n2[h][:, :, 0])

        def root(h):
            nc.scalar.activation(out=inv_n[h][:], in_=inv_n2[h][:], func=ACT.Sqrt)

        def make_factor_a(h):
            nc.vector.scalar_tensor_tensor(out=factor_a[h][:], in0=inv_n[h][:], scalar=-1.0, in1=m_sb[:, h, :],
                                           op0=ALU.mult, op1=ALU.mult)

        v_words = {}

        def turn_v(r):
            h, u = divmod(r, 2)
            words = v_sb[h][:].rearrange("p n o -> p (n o)").bitcast(F32)
            for a in range(2):
                v_words[r, a] = bank(4 + 2 * ((r + 1) % 2) + a, "v_words", [P, HALF], F32)
                for n in range(HALF // P):
                    first = (a * (HALF // P) + n) * (K_PASS // 2)
                    nc.tensor.transpose(v_words[r, a][:, n * P:(n + 1) * P],
                                        words[:, first + u:first + K_PASS // 2:2], identity[:])

        def v_t(j, a):
            return v_words[j // 2, a][:].bitcast(BF16)[:, j % 2:2 * HALF:2]

        scaled = {}

        def scale_tile(j):
            h, t = divmod(j, PACK)
            scaled[j] = rotating("scaled", SCALED_SLOTS, [P, DI], F32)
            for a in range(2):
                nc.scalar.activation(out=scaled[j][:, half(a)], in_=gw[j, a][:], func=ACT.Copy,
                                     scale=factor_a[h][:, t:t + 1])

        def project(j, a):
            h, t = divmod(j, PACK)
            summands = rotating("summands", 2, [P, HALF], F32)
            nc.vector.scalar_tensor_tensor(out=summands[:], in0=v_t(j, a), scalar=inv_n2[h][:, t:t + 1],
                                           in1=scaled[j][:, half(a)], op0=ALU.mult, op1=ALU.mult,
                                           accum_out=half_sums[:, j, a:a + 1])

        def join(j):
            nc.vector.tensor_scalar(out=factor_w[:, j:j + 1], in0=half_sums[:, j, 0:1], scalar1=half_sums[:, j, 1:2],
                                    scalar2=None, op0=ALU.add)

        def chunks(ap):
            return ap.rearrange("p (c i) -> p c i", i=QUARTER)

        def combine(j, c, count):
            h, t = divmod(j, PACK)
            a, within = divmod(c, 2)
            nc.vector.scalar_tensor_tensor(out=dv[h][:, c:c + count, t, :],
                                           in0=chunks(v_t(j, a)[:, within * QUARTER:(within + count) * QUARTER]),
                                           scalar=factor_w[:, j:j + 1],
                                           in1=chunks(scaled[j][:, c * QUARTER:(c + count) * QUARTER]),
                                           op0=ALU.mult, op1=ALU.subtract)

        def combine_half(j, a):
            combine(j, 2 * a, 2)

        def combine_half_off_vector(j, a):
            h, t = divmod(j, PACK)
            along_v = rotating("along_v", 1, [P, HALF], F32)
            nc.scalar.activation(out=along_v[:], in_=v_t(j, a), func=ACT.Copy, scale=factor_w[:, j:j + 1])
            nc.gpsimd.tensor_tensor(out=dv[h][:, 2 * a:2 * a + 2, t, :], in0=chunks(along_v[:]),
                                    in1=chunks(scaled[j][:, half(a)]), op=ALU.subtract)

        def project_pair(r):
            j = 2 * r
            project(j, 0)
            project(j, 1)
            project(j + 1, 0)
            join(j)
            project(j + 1, 1)

        dv_pieces = {}

        def interleave_dv(copy, h, c):
            dv_pieces[h, c] = piece()
            interleave(copy, dv[h][:, c], dv_pieces[h, c])

        def interleave_dv_on_gpsimd(h, c):
            dv_pieces[h, c] = turn_piece()
            on_gpsimd(dv_pieces[h, c][:].rearrange("p (i t) -> p i t", t=PACK), dv[h][:, c].rearrange("p t i -> p i t"))

        def quantize_dv(h, c):
            rows = slice(c * QUARTER, (c + 1) * QUARTER)
            quantize(dv_codes[h][:, rows], dv_scales[h][:, rows], dv_pieces[h, c][:])

        def turn_b():
            words = b_sb[:].rearrange("p n o -> p (n o)").bitcast(F32)
            interleaved = rotating("wide", WIDE_SLOTS, [P, COLUMN_PASSES * R * PACK], BF16)
            interleaved_words = interleaved[:].bitcast(F32)
            for h in range(COLUMN_PASSES):
                b_words = bank(h, "b_words", [P, R // P, 2, P], F32)
                for n in range(R // P):
                    for u in range(2):
                        first = n * (DO // 2) + h * (K_PASS // 2)
                        nc.tensor.transpose(b_words[:, n, u, :], words[:, first + u:first + K_PASS // 2:2], identity[:])
                on_scalar(interleaved_words[:, h * 2 * R:(h + 1) * 2 * R].rearrange("p (n row u) -> p n row u", n=R // P, u=2),
                          b_words[:].rearrange("p n u row -> p n row u"))
            return interleaved

        out_sums = {}

        def second_product(n, h):
            if h == 0:
                out_sums[n] = bank(OUT_BANKS[n], "out_sums", [P, R], F32)
            rows = slice(n * P, (n + 1) * P)
            columns = slice(h * R, (h + 1) * R)
            nc.tensor.matmul_mx(out=out_sums[n][:],
                                lhsT=dv_codes[h][:, rows].bitcast(FP8X4), lhsT_scale=dv_scales[h][:, rows],
                                rhs=b_codes[:, columns].bitcast(FP8X4), rhs_scale=b_scales[:, columns],
                                start=(h == 0), stop=(h == COLUMN_PASSES - 1))

        def finish(c, copies):
            for n, copy in zip((2 * c, 2 * c + 1), copies):
                second_product(n, 1)
                result = rotating("result", ROW_TILES, [P, R], F32)
                copy(result[:], out_sums[n][:])
                nc.sync.dma_start(out=out[n * P:(n + 1) * P, :], in_=result[:])

        widened = [widen(0, 0), widen(0, 1)]
        x_halves = [interleave_x(widened[0]), interleave_x(widened[1])]
        quantize_x(0, 0, x_halves[0])
        interleave_g(on_vector, 0, 0, piece())
        quantize_x(0, 1, x_halves[1])
        quantize_g(0, 0)
        first_pair_pass(0)
        gram_blocks(0)
        for q in range(1, TOKEN_PASSES):
            widened = [widen(q, 0), widen(q, 1)]
            first_half = interleave_x(widened[0])
            if q < LAST:
                interleave_g(on_vector, 0, q, piece())
            else:
                interleave_g(on_scalar, 0, q, piece())
                root(0)
            quantize_x(q, 0, first_half)
            if q == LAST - 1:
                take_diagonal(0)
            second_half = interleave_x(widened[1])
            quantize_g(0, q)
            if q == LAST:
                make_factor_a(0)
            quantize_x(q, 1, second_half)
            if q == LAST - 1:
                invert_n2(0)
            first_pair_pass(q)
            if q == 1:
                turn_v(0)
            if q == LAST - 1:
                gram_blocks(1)

        for q in range(LAST):
            interleave_g(on_scalar, 1, q, piece())
        take_diagonal(1)
        interleave_g(on_vector, 1, LAST, turn_piece())
        quantize_pair(1)
        scale_tile(0)
        scale_tile(1)
        invert_n2(1)
        root(1)
        product_tile(2)
        turn_v(1)
        product_tile(3)
        for r in range(2):
            j = 2 * r
            interleave_g_on_gpsimd(r + 2, LAST)
            for q in range(LAST):
                interleave_g(on_scalar, r + 2, q, piece())
            if r == 0:
                scale_tile(2)
                scale_tile(3)
            project_pair(r)
            combine_half(j, 0)
            join(j + 1)
            combine_half(j, 1)
            if r == 0:
                make_factor_a(1)
            quantize_pair(r + 2)
            combine_half(j + 1, 0)
            combine_half(j + 1, 1)
            if r == 1:
                scale_tile(4)
                scale_tile(5)
            product_tile(j + 4)
            turn_v(r + 2)
            product_tile(j + 5)

        interleave_dv_on_gpsimd(0, 0)
        interleave_dv(on_scalar, 0, 1)
        scale_tile(6)
        interleave_dv(on_scalar, 0, 2)
        project_pair(2)
        combine_half(4, 0)
        join(5)
        quantize_dv(0, 1)
        quantize_dv(0, 0)
        combine_half(4, 1)
        combine_half(5, 0)
        scale_tile(7)
        combine_half_off_vector(5, 1)
        interleave_dv(on_scalar, 0, 3)
        b_interleaved = turn_b()

        project_pair(3)
        quantize_dv(0, 2)
        join(7)
        for c in range(DI // QUARTER):
            combine(6, c, 1)
            combine(7, c, 1)
            if c < 3:
                interleave_dv(on_scalar, 1, c)
            if c == 0:
                quantize_dv(0, 3)
                quantize(b_codes[:], b_scales[:], b_interleaved[:])
                for n in range(EARLY_OUT_TILES):
                    second_product(n, 0)
            if c == 2:
                quantize_dv(1, 0)
        finish(0, (on_scalar, on_scalar))
        for n in range(EARLY_OUT_TILES, ROW_TILES):
            second_product(n, 0)
        quantize_dv(1, 1)
        interleave_dv(on_vector, 1, 3)
        quantize_dv(1, 2)
        quantize_dv(1, 3)
        for c in range(1, DI // QUARTER):
            finish(c, (on_scalar, on_vector))
